import numpy as np
import ml_dtypes


def mxq(x, axis, fmt="e4m3"):
    dtype, down = {"e4m3": (ml_dtypes.float8_e4m3fn, 7), "e5m2": (ml_dtypes.float8_e5m2, 14)}[fmt]
    v = np.moveaxis(np.asarray(x, np.float32).astype(ml_dtypes.bfloat16).astype(np.float64), axis, -1)
    blocks = v.reshape(v.shape[:-1] + (-1, 32))
    amax = np.abs(blocks).max(-1, keepdims=True)
    byte = np.maximum(np.where(amax > 0, np.frexp(amax)[1] - 1 + 127, 0) - down, 1)
    scale = np.exp2(byte - 127.0)
    codes = (blocks / scale).astype(np.float32).astype(dtype).astype(np.float64)
    return np.moveaxis((codes * scale).reshape(v.shape), -1, axis)


WIDE = False


def mx_kscale(k):
    if not WIDE:
        return np.ones(k)
    levels = np.array([10, -10, 5, -5, 0])
    if k % 512:
        return np.exp2(np.random.permutation(np.resize(levels, k // 32))).repeat(32)
    a = np.empty((k // 512, 16))
    for p in range(k // 512):
        a[p, :8] = np.random.permutation(np.resize(levels, 8))
        for g in range(8):
            far = levels[np.abs(levels - a[p, g]) >= 10]
            a[p, g + 8] = far[np.random.randint(len(far))]
    return np.exp2(a.ravel()).repeat(32)


def f64(x):
    return np.asarray(x).astype(np.float64)


def striped(idx):
    return np.tile(np.asarray(idx).reshape(-1, 16).T, (8, 1)).astype(np.uint16)


def unstriped(offs):
    return offs[:16].T.reshape(-1).astype(np.int64)


E2M1 = np.array([0.0, 0.5, 1.0, 1.5, 2.0, 3.0, 4.0, 6.0, -0.0, -0.5, -1.0, -1.5, -2.0, -3.0, -4.0, -6.0])


def pack_weight(w, fmt):
    k, n = w.shape
    w = f64(np.asarray(w, np.float32).astype(ml_dtypes.bfloat16)).reshape(k // 32, 32, n)
    amax = np.abs(w).max(1)
    if fmt == "e4m3":
        byte = np.frexp(amax)[1] - 1 + 127 - 7
    else:
        mant, ex = np.frexp(amax / 6.0)
        byte = np.where(mant > 0.5, ex, ex - 1) + 127
    byte = np.clip(np.where(amax > 0, byte, 1), 1, 254)
    scaled = (w * np.exp2(127.0 - byte)[:, None, :]).reshape(k, n).astype(np.float32)
    by_word = np.ascontiguousarray(scaled.reshape(k // 512, 128, 4, n).transpose(0, 1, 3, 2))
    if fmt == "e4m3":
        words = by_word.astype(ml_dtypes.float8_e4m3fn).view(np.uint8)
    else:
        c = by_word.astype(ml_dtypes.float4_e2m1fn).view(np.uint8) & 0xF
        words = (c[..., 0::2] | (c[..., 1::2] << 4)).reshape(k // 512, 128, 2 * n)
    return np.ascontiguousarray(words), np.ascontiguousarray(byte.astype(np.uint8).reshape(k // 512, 16, n))


def unpack_weight(words, scales, fmt):
    g, _, n = scales.shape
    words = np.ascontiguousarray(words).reshape(g, 128, n, -1)
    if fmt == "e4m3":
        vals = words.view(ml_dtypes.float8_e4m3fn).astype(np.float64)
    else:
        nib = np.empty((g, 128, n, 4), np.uint8)
        nib[..., 0::2] = words & 0xF
        nib[..., 1::2] = words >> 4
        vals = E2M1[nib]
    vals = vals * np.repeat(np.exp2(scales.astype(np.float64) - 127.0), 8, axis=1)[..., None]
    return vals.transpose(0, 1, 3, 2).reshape(g * 512, n)


def bf(x):
    return np.asarray(x, np.float32).astype(ml_dtypes.bfloat16)


def planes(Y):
    r, m = Y.shape
    b = f64(bf(Y)).reshape(r // 32, 32, m)
    amax = np.abs(b).max(1)
    byte = np.clip(np.where(amax > 0, np.frexp(amax)[1] - 1 + 127 - 7, 1), 1, 254)
    codes = (b * np.exp2(127.0 - byte)[:, None, :]).reshape(r, m).astype(np.float32).astype(ml_dtypes.float8_e4m3fn).view(np.uint8)
    words = codes.reshape(r // 512, 128, 4, m).transpose(0, 1, 3, 2)
    return np.ascontiguousarray(words), np.ascontiguousarray(byte.astype(np.uint8).reshape(r // 512, 16, m))


D, K, U, V, T, I, Q, E = 512, 512, 1024, 1024, 2048, 512, 256, 512


def setup_inputs():
    n = np.random.standard_normal
    idx = np.random.randint(0, U, I)
    idx2 = np.random.randint(0, V, I)
    idx3 = np.random.permutation(T)[:I]
    fd = mx_kscale(D)
    fk = mx_kscale(K)
    fi = mx_kscale(I)
    ti = np.ones(T)
    ti[idx3] = fi
    sub1p = pack_weight(n((D, U)) / fd[:, None], "e2m1")
    sub2p = pack_weight(n((K, V)) / fk[:, None], "e4m3")
    return {
        "query": (n((D, Q)) * 0.4 / np.sqrt(D) * fd[:, None]).astype(np.float32),
        "query2": (n((K, Q)) * 0.4 / np.sqrt(K) * fk[:, None]).astype(np.float32),
        "sub1_words": sub1p[0],
        "sub1_scales": sub1p[1],
        "sub2_words": sub2p[0],
        "sub2_scales": sub2p[1],
        "size": (np.random.uniform(0.5, 2.0, (1, I)) * fi).astype(np.float32),
        "vals": (n((E, T)) / ti).astype(np.float32),
        "offs": striped(idx),
        "offs2": striped(idx2),
        "offs3": striped(idx3),
    }


def reference(query, query2, sub1_words, sub1_scales, sub2_words, sub2_scales, size, vals, offs, offs2, offs3):
    idx = unstriped(offs)
    idx2 = unstriped(offs2)
    idx3 = unstriped(offs3)
    sub1u = unpack_weight(sub1_words, sub1_scales, "e2m1")
    sub2u = unpack_weight(sub2_words, sub2_scales, "e4m3")
    queryq = mxq(f64(query), 0, "e4m3")
    b = queryq.T @ sub1u
    query2q = mxq(f64(query2), 0, "e4m3")
    r = query2q.T @ sub2u
    a = b[:, idx] + r[:, idx2]
    p = np.exp(a - np.max(a, axis=1, keepdims=True))
    w = p * f64(size) / np.sum(p, axis=1, keepdims=True)
    wt = w.T
    vt = f64(vals)[:, idx3].T
    vtq = mxq(vt, 0, "e4m3")
    wtq = mxq(wt, 0, "e4m3")
    o = vtq.T @ wtq
    words, scales = planes(o)
    return o, words, scales

@@ -1,0 +1,207 @@
+from contextlib import ExitStack
+
+import concourse.mybir as mybir
+from concourse.masks import make_identity
+
+D, K, U, V, T, I, Q, E = 512, 512, 1024, 1024, 2048, 512, 256, 512
+FLOPS = 2 * D * Q * U + 2 * K * Q * V + 2 * I * E * Q
+
+F32 = mybir.dt.float32
+BF16 = mybir.dt.bfloat16
+I32 = mybir.dt.int32
+U32 = mybir.dt.uint32
+U16 = mybir.dt.uint16
+U8 = mybir.dt.uint8
+FP8X4 = mybir.dt.float8_e4m3fn_x4
+FP4X4 = mybir.dt.float4_e2m1fn_x4
+ALU = mybir.AluOpType
+ACT = mybir.ActivationFunctionType
+AXIS = mybir.AxisListType
+
+P = 128
+PACK = 4
+BANK = 512
+HALVES = Q // P
+
+
+def tile_attend_productkeys_pl_kernel(
+    tc, query, query2, sub1_words, sub1_scales, sub2_words, sub2_scales, size, vals, offs, offs2, offs3,
+    out_0, out_1, out_2,
+):
+    nc = tc.nc
+    with ExitStack() as ctx:
+        keep = ctx.enter_context(tc.tile_pool(name="keep", bufs=1))
+        sums = ctx.enter_context(tc.psum_pool(name="sums", bufs=4))
+        turns = ctx.enter_context(tc.psum_pool(name="turns", bufs=3))
+        spread = ctx.enter_context(tc.psum_pool(name="spread", bufs=1))
+
+        def tile(shape, dtype, name):
+            return keep.tile(shape, dtype, name=name, align_bytes=64)
+
+        q_raw = [tile([P, PACK, Q], F32, f"q_raw{n}") for n in range(2)]
+        book1 = tile([P, 2 * U], U8, "book1")
+        book2 = tile([P, V], U32, "book2")
+        book_scales = [tile([P, U], U8, f"book_scales{n}") for n in range(2)]
+        lists = [keep.tile([P, I // 16], U16, name=f"list{n}") for n in range(3)]
+        pool_rows = [tile([P, T], F32, f"pool_rows{t}") for t in range(PACK)]
+        size_cols = tile([P, PACK], F32, "size_cols")
+        vals_by_place = vals.rearrange("(p t) n -> t p n", t=PACK)
+
+        def load_scales(queue, plane, rows):
+            for quad in range(4):
+                queue.dma_start(
+                    out=plane[32 * quad : 32 * quad + 4, :].bitcast(I32),
+                    in_=rows[0, 4 * quad : 4 * quad + 4, :].bitcast(I32),
+                )
+
+        nc.sync.dma_start(out=q_raw[0][:], in_=query.rearrange("(p t) q -> p t q", t=PACK))
+        nc.sync.dma_start(out=book1[:].bitcast(I32), in_=sub1_words[0].bitcast(I32))
+        load_scales(nc.sync, book_scales[0], sub1_scales)
+        nc.sync.dma_start(out=q_raw[1][:], in_=query2.rearrange("(p t) q -> p t q", t=PACK))
+        nc.sync.dma_start(out=book2[:].bitcast(I32), in_=sub2_words[0].rearrange("p n t -> p (n t)").bitcast(I32))
+        load_scales(nc.sync, book_scales[1], sub2_scales)
+        nc.sync.dma_start(lists[0][:], offs)
+        nc.sync.dma_start(out=pool_rows[0][:], in_=vals_by_place[0])
+        nc.sync.dma_start(lists[1][:], offs2)
+        nc.sync.dma_start(lists[2][:], offs3)
+        nc.sync.dma_start(out=pool_rows[1][:], in_=vals_by_place[1])
+        nc.sync.dma_start(out=size_cols[:], in_=size.rearrange("o (p t) -> p (o t)", t=PACK))
+        for t in range(2, PACK):
+            nc.sync.dma_start(out=pool_rows[t][:], in_=vals_by_place[t])
+
+        ident = tile([P, P], F32, "ident")
+        make_identity(nc, ident[:])
+        warm = tile([P, 1], F32, "warm")
+        nc.scalar.activation(out=warm[:], in_=ident[:, 0:1], func=ACT.Exp)
+
+        q_codes, q_scales = [], []
+        for n in range(2):
+            grouped = tile([P, Q, PACK], BF16, f"q_grouped{n}")
+            nc.vector.tensor_copy(
+                out=grouped[:].rearrange("p (c i) t -> p c t i", i=4),
+                in_=q_raw[n][:].rearrange("p t (c i) -> p c t i", i=4),
+            )
+            codes = tile([P, Q], U32, f"q_codes{n}")
+            scales = tile([P, Q], U8, f"q_scales{n}")
+            nc.vector.quantize_mx(
+                out=codes[:].bitcast(FP8X4), scales=scales[:], in_=grouped[:].rearrange("p q t -> p (q t)")
+            )
+            q_codes.append(codes)
+            q_scales.append(scales)
+
+        scores = {}
+        for n in range(2):
+            for h in range(HALVES):
+                rows = slice(h * P, (h + 1) * P)
+                whole = tile([P, U], F32, f"scores{n}_{h}")
+                for c in range(U // BANK):
+                    cols = slice(c * BANK, (c + 1) * BANK)
+                    if n == 0:
+                        keys = book1[:, 2 * c * BANK : 2 * (c + 1) * BANK].bitcast(FP4X4)
+                    else:
+                        keys = book2[:, cols].bitcast(FP8X4)
+                    bank = sums.tile([P, BANK], F32, name="bank")
+                    nc.tensor.matmul_mx(
+                        out=bank[:], lhsT=q_codes[n][:, rows].bitcast(FP8X4), lhsT_scale=q_scales[n][:, rows],
+                        rhs=keys, rhs_scale=book_scales[n][:, cols], start=True, stop=True,
+                    )
+                    nc.scalar.copy(out=whole[:, cols], in_=bank[:])
+                scores[n, h] = whole
+
+        size_bank = spread.tile([P, PACK, P], F32, name="size_bank")
+        for t in range(PACK):
+            nc.tensor.transpose(size_bank[:, t, :], size_cols[:, t : t + 1].to_broadcast([P, P]), ident[:])
+
+        def turn_and_quantise(rows_bf16, codes, scales, name):
+            words = rows_bf16[:].bitcast(F32)
+            turned = turns.tile([P, 2, P], F32, name="turned")
+            for u in range(2):
+                nc.tensor.transpose(turned[:, u, :], words[:, u : I // 2 : 2], ident[:])
+            grouped = tile([P, P * PACK], BF16, name)
+            nc.scalar.copy(
+                out=grouped[:].bitcast(F32).rearrange("p (c u) -> p c u", u=2),
+                in_=turned[:].rearrange("p u c -> p c u"),
+            )
+            nc.vector.quantize_mx(out=codes.bitcast(FP8X4), scales=scales, in_=grouped[:])
+
+        v_codes = tile([P, E], U32, "v_codes")
+        v_scales = tile([P, E], U8, "v_scales")
+        w_codes = tile([P, Q], U32, "w_codes")
+        w_scales = tile([P, Q], U8, "w_scales")
+
+        def values(t):
+            picked = tile([P, I], BF16, f"picked{t}")
+            nc.vector.tensor_copy(out=picked[:], in_=pool_rows[t][:].indirect(lists[2][:]))
+            cols = slice(t * P, (t + 1) * P)
+            turn_and_quantise(picked, v_codes[:, cols], v_scales[:, cols], f"v_grouped{t}")
+
+        first = []
+        for h in range(HALVES):
+            picked_b = tile([P, I], F32, f"picked_b{h}")
+            nc.vector.tensor_copy(out=picked_b[:], in_=scores[0, h][:].indirect(lists[0][:]))
+            first.append(picked_b)
+
+        def weights(h):
+            logits = tile([P, I], F32, f"logits{h}")
+            nc.vector.tensor_tensor(out=logits[:], in0=scores[1, h][:].indirect(lists[1][:]), in1=first[h][:], op=ALU.add)
+            neg_max = tile([P, 1], F32, f"neg_max{h}")
+            nc.vector.tensor_reduce(out=neg_max[:], in_=logits[:], axis=AXIS.X, op=ALU.max, negate=True)
+            expd = tile([P, I], F32, f"expd{h}")
+            total = tile([P, 1], F32, f"total{h}")
+            nc.scalar.activation(out=expd[:], in_=logits[:], func=ACT.Exp, bias=neg_max[:], scale=1.0, accum_out=total[:])
+            inv = tile([P, 1], F32, f"inv{h}")
+            nc.vector.reciprocal(out=inv[:], in_=total[:])
+            w = tile([P, I], BF16, f"w{h}")
+            nc.vector.scalar_tensor_tensor(
+                out=w[:].rearrange("p (s t) -> p s t", t=PACK),
+                in0=expd[:].rearrange("p (s t) -> p s t", t=PACK),
+                scalar=inv[:], in1=size_bank[:].rearrange("p t s -> p s t"), op0=ALU.mult, op1=ALU.mult,
+            )
+            cols = slice(h * P, (h + 1) * P)
+            turn_and_quantise(w, w_codes[:, cols], w_scales[:, cols], f"w_grouped{h}")
+
+        o_codes = tile([P, Q], U32, "o_codes")
+        o_scales = tile([P, Q], U8, "o_scales")
+        out_rows = out_0.rearrange("(p t) q -> p t q", t=PACK)
+        out_words = out_1[0].rearrange("p c t -> p (c t)").bitcast(I32)
+
+        o_sb = tile([P, PACK, Q], F32, "o_sb")
+        o_grouped = tile([P, Q, PACK], BF16, "o_grouped")
+        o_banks = [sums.tile([P, PACK, P], F32, name="bank") for h in range(HALVES)]
+        last = PACK - 1
+
+        def product(h, t):
+            cols = slice(h * P, (h + 1) * P)
+            feats = slice(t * P, (t + 1) * P)
+            nc.tensor.matmul_mx(
+                out=o_banks[h][:, t, :], lhsT=v_codes[:, feats].bitcast(FP8X4), lhsT_scale=v_scales[:, feats],
+                rhs=w_codes[:, cols].bitcast(FP8X4), rhs_scale=w_scales[:, cols], start=True, stop=True,
+            )
+
+        weights(0)
+        weights(1)
+        for t in range(last):
+            values(t)
+        for h in range(HALVES):
+            for t in range(last):
+                product(h, t)
+            nc.scalar.copy(out=o_sb[:, :last, h * P : (h + 1) * P], in_=o_banks[h][:, :last, :])
+        nc.sync.dma_start(out=out_rows[:, :last, :], in_=o_sb[:, :last, :])
+        values(last)
+        for h in range(HALVES):
+            product(h, last)
+        nc.vector.tensor_copy(out=o_grouped[:, :P, :], in_=o_banks[0][:].rearrange("p t q -> p q t"))
+        nc.scalar.copy(out=o_grouped[:, P:, :], in_=o_banks[1][:].rearrange("p t q -> p q t"))
+        nc.vector.quantize_mx(
+            out=o_codes[:].bitcast(FP8X4), scales=o_scales[:], in_=o_grouped[:].rearrange("p q t -> p (q t)")
+        )
+        for h in range(HALVES):
+            nc.scalar.copy(out=o_sb[:, last, h * P : (h + 1) * P], in_=o_banks[h][:, last, :])
+        nc.scalar.dma_start(out=out_rows[:, last, :], in_=o_sb[:, last, :])
+        nc.sync.dma_start(out=out_words, in_=o_codes[:].bitcast(I32))
+        for quad in range(4):
+            queue = nc.sync if quad % 2 == 0 else nc.scalar
+            queue.dma_start(
+                out=out_2[0, 4 * quad : 4 * quad + 4, :].bitcast(I32),
+                in_=o_scales[32 * quad : 32 * quad + 4, :].bitcast(I32),
+            )

@@ -35,8 +35,8 @@ def tile_attend_productkeys_pl_kernel(
         turns = ctx.enter_context(tc.psum_pool(name="turns", bufs=3))
         spread = ctx.enter_context(tc.psum_pool(name="spread", bufs=1))
 
-        def tile(shape, dtype, name):
-            return keep.tile(shape, dtype, name=name, align_bytes=64)
+        def tile(shape, dtype, name, tag=None):
+            return keep.tile(shape, dtype, name=name, tag=tag or name, align_bytes=64)
 
         q_raw = [tile([P, PACK, Q], F32, f"q_raw{n}") for n in range(2)]
         book1 = tile([P, 2 * U], U8, "book1")
@@ -63,10 +63,9 @@ def tile_attend_productkeys_pl_kernel(
         nc.sync.dma_start(lists[0][:], offs)
         nc.sync.dma_start(out=pool_rows[0][:], in_=vals_by_place[0])
         nc.sync.dma_start(lists[1][:], offs2)
-        nc.sync.dma_start(lists[2][:], offs3)
-        nc.sync.dma_start(out=pool_rows[1][:], in_=vals_by_place[1])
         nc.sync.dma_start(out=size_cols[:], in_=size.rearrange("o (p t) -> p (o t)", t=PACK))
-        for t in range(2, PACK):
+        nc.sync.dma_start(lists[2][:], offs3)
+        for t in range(1, PACK):
             nc.sync.dma_start(out=pool_rows[t][:], in_=vals_by_place[t])
 
         ident = tile([P, P], F32, "ident")
@@ -77,15 +76,20 @@ def tile_attend_productkeys_pl_kernel(
         q_codes, q_scales = [], []
         for n in range(2):
             grouped = tile([P, Q, PACK], BF16, f"q_grouped{n}")
-            nc.vector.tensor_copy(
-                out=grouped[:].rearrange("p (c i) t -> p c t i", i=4),
-                in_=q_raw[n][:].rearrange("p t (c i) -> p c t i", i=4),
-            )
             codes = tile([P, Q], U32, f"q_codes{n}")
             scales = tile([P, Q], U8, f"q_scales{n}")
-            nc.vector.quantize_mx(
-                out=codes[:].bitcast(FP8X4), scales=scales[:], in_=grouped[:].rearrange("p q t -> p (q t)")
-            )
+            for h in range(HALVES):
+                rows = slice(h * P, (h + 1) * P)
+                nc.vector.tensor_copy(
+                    out=grouped[:, rows, :].rearrange("p (c i) t -> p c t i", i=4),
+                    in_=q_raw[n][:, :, rows].rearrange("p t (c i) -> p c t i", i=4),
+                )
+            for h in range(HALVES):
+                rows = slice(h * P, (h + 1) * P)
+                nc.vector.quantize_mx(
+                    out=codes[:, rows].bitcast(FP8X4), scales=scales[:, rows],
+                    in_=grouped[:, rows, :].rearrange("p q t -> p (q t)"),
+                )
             q_codes.append(codes)
             q_scales.append(scales)
 
@@ -105,35 +109,39 @@ def tile_attend_productkeys_pl_kernel(
                         out=bank[:], lhsT=q_codes[n][:, rows].bitcast(FP8X4), lhsT_scale=q_scales[n][:, rows],
                         rhs=keys, rhs_scale=book_scales[n][:, cols], start=True, stop=True,
                     )
-                    nc.scalar.copy(out=whole[:, cols], in_=bank[:])
+                    if (n, h, c) == (0, 0, 1):
+                        nc.vector.tensor_copy(out=whole[:, cols], in_=bank[:])
+                    else:
+                        nc.scalar.copy(out=whole[:, cols], in_=bank[:])
                 scores[n, h] = whole
 
         size_bank = spread.tile([P, PACK, P], F32, name="size_bank")
         for t in range(PACK):
             nc.tensor.transpose(size_bank[:, t, :], size_cols[:, t : t + 1].to_broadcast([P, P]), ident[:])
 
-        def turn_and_quantise(rows_bf16, codes, scales, name):
+        def turn(rows_bf16, grouped):
             words = rows_bf16[:].bitcast(F32)
             turned = turns.tile([P, 2, P], F32, name="turned")
             for u in range(2):
                 nc.tensor.transpose(turned[:, u, :], words[:, u : I // 2 : 2], ident[:])
-            grouped = tile([P, P * PACK], BF16, name)
             nc.scalar.copy(
-                out=grouped[:].bitcast(F32).rearrange("p (c u) -> p c u", u=2),
+                out=grouped.bitcast(F32).rearrange("p (c u) -> p c u", u=2),
                 in_=turned[:].rearrange("p u c -> p c u"),
             )
-            nc.vector.quantize_mx(out=codes.bitcast(FP8X4), scales=scales, in_=grouped[:])
 
-        v_codes = tile([P, E], U32, "v_codes")
-        v_scales = tile([P, E], U8, "v_scales")
-        w_codes = tile([P, Q], U32, "w_codes")
-        w_scales = tile([P, Q], U8, "w_scales")
+        early = tile([P, 4 * I], BF16, "early")
+        v_last = tile([P, I], BF16, "v_last")
+        w_last = tile([P, I], BF16, "w_last")
 
         def values(t):
             picked = tile([P, I], BF16, f"picked{t}")
-            nc.vector.tensor_copy(out=picked[:], in_=pool_rows[t][:].indirect(lists[2][:]))
-            cols = slice(t * P, (t + 1) * P)
-            turn_and_quantise(picked, v_codes[:, cols], v_scales[:, cols], f"v_grouped{t}")
+            if t == 0:
+                rounded = tile([P, T], BF16, "rounded")
+                nc.scalar.activation(out=rounded[:], in_=pool_rows[t][:], func=ACT.Copy)
+                nc.scalar.activation(out=picked[:], in_=rounded[:].indirect(lists[2][:]), func=ACT.Copy)
+            else:
+                nc.vector.tensor_copy(out=picked[:], in_=pool_rows[t][:].indirect(lists[2][:]))
+            turn(picked, early[:, t * I : (t + 1) * I] if t < PACK - 1 else v_last[:])
 
         first = []
         for h in range(HALVES):
@@ -141,67 +149,78 @@ def tile_attend_productkeys_pl_kernel(
             nc.vector.tensor_copy(out=picked_b[:], in_=scores[0, h][:].indirect(lists[0][:]))
             first.append(picked_b)
 
-        def weights(h):
-            logits = tile([P, I], F32, f"logits{h}")
-            nc.vector.tensor_tensor(out=logits[:], in0=scores[1, h][:].indirect(lists[1][:]), in1=first[h][:], op=ALU.add)
-            neg_max = tile([P, 1], F32, f"neg_max{h}")
-            nc.vector.tensor_reduce(out=neg_max[:], in_=logits[:], axis=AXIS.X, op=ALU.max, negate=True)
-            expd = tile([P, I], F32, f"expd{h}")
-            total = tile([P, 1], F32, f"total{h}")
-            nc.scalar.activation(out=expd[:], in_=logits[:], func=ACT.Exp, bias=neg_max[:], scale=1.0, accum_out=total[:])
-            inv = tile([P, 1], F32, f"inv{h}")
-            nc.vector.reciprocal(out=inv[:], in_=total[:])
-            w = tile([P, I], BF16, f"w{h}")
+        logits = tile([P, HALVES, I], F32, "logits")
+        for h in range(HALVES):
+            nc.vector.tensor_tensor(
+                out=logits[:, h, :], in0=scores[1, h][:].indirect(lists[1][:]), in1=first[h][:], op=ALU.add
+            )
+        neg_max = tile([P, HALVES], F32, "neg_max")
+        nc.vector.tensor_reduce(out=neg_max[:], in_=logits[:], axis=AXIS.X, op=ALU.max, negate=True)
+
+        for t in range(PACK - 1):
+            values(t)
+        expd = [tile([P, I], F32, "expd0", tag="rounded"), tile([P, I], F32, "expd1")]
+        total = tile([P, HALVES], F32, "total")
+        for h in range(HALVES):
+            nc.scalar.activation(
+                out=expd[h][:], in_=logits[:, h, :], func=ACT.Exp, bias=neg_max[:, h : h + 1], scale=1.0,
+                accum_out=total[:, h : h + 1],
+            )
+        inv = tile([P, HALVES], F32, "inv", tag="pool_rows2")
+        nc.vector.reciprocal(out=inv[:], in_=total[:])
+
+        def weights(h, w, grouped):
             nc.vector.scalar_tensor_tensor(
                 out=w[:].rearrange("p (s t) -> p s t", t=PACK),
-                in0=expd[:].rearrange("p (s t) -> p s t", t=PACK),
-                scalar=inv[:], in1=size_bank[:].rearrange("p t s -> p s t"), op0=ALU.mult, op1=ALU.mult,
+                in0=expd[h][:].rearrange("p (s t) -> p s t", t=PACK),
+                scalar=inv[:, h : h + 1], in1=size_bank[:].rearrange("p t s -> p s t"), op0=ALU.mult, op1=ALU.mult,
             )
-            cols = slice(h * P, (h + 1) * P)
-            turn_and_quantise(w, w_codes[:, cols], w_scales[:, cols], f"w_grouped{h}")
+            turn(w, grouped)
+
+        weights(0, tile([P, I], BF16, "w0"), early[:, 3 * I :])
+        values(PACK - 1)
+        w1 = tile([P, I], BF16, "w1", tag="pool_rows3")
+        weights(1, w1, w_last[:])
+
+        def quantise(grouped, name, tag=None):
+            width = grouped.shape[1] // PACK
+            codes = tile([P, width], U32, name + "_codes", tag=tag)
+            scales = tile([P, width], U8, name + "_scales")
+            nc.vector.quantize_mx(out=codes[:].bitcast(FP8X4), scales=scales[:], in_=grouped[:])
+            return [(codes[:, c : c + P].bitcast(FP8X4), scales[:, c : c + P]) for c in range(0, width, P)]
+
+        early_mx = quantise(early, "early", tag="expd1")
+        v_mx = early_mx[:3] + quantise(v_last, "v_last")
+        w_mx = early_mx[3:] + quantise(w_last, "w_last")
 
         o_codes = tile([P, Q], U32, "o_codes")
         o_scales = tile([P, Q], U8, "o_scales")
         out_rows = out_0.rearrange("(p t) q -> p t q", t=PACK)
         out_words = out_1[0].rearrange("p c t -> p (c t)").bitcast(I32)
-
-        o_sb = tile([P, PACK, Q], F32, "o_sb")
         o_grouped = tile([P, Q, PACK], BF16, "o_grouped")
-        o_banks = [sums.tile([P, PACK, P], F32, name="bank") for h in range(HALVES)]
-        last = PACK - 1
-
-        def product(h, t):
+        for h in range(HALVES):
             cols = slice(h * P, (h + 1) * P)
-            feats = slice(t * P, (t + 1) * P)
-            nc.tensor.matmul_mx(
-                out=o_banks[h][:, t, :], lhsT=v_codes[:, feats].bitcast(FP8X4), lhsT_scale=v_scales[:, feats],
-                rhs=w_codes[:, cols].bitcast(FP8X4), rhs_scale=w_scales[:, cols], start=True, stop=True,
-            )
-
-        weights(0)
-        weights(1)
-        for t in range(last):
-            values(t)
-        for h in range(HALVES):
-            for t in range(last):
-                product(h, t)
-            nc.scalar.copy(out=o_sb[:, :last, h * P : (h + 1) * P], in_=o_banks[h][:, :last, :])
-        nc.sync.dma_start(out=out_rows[:, :last, :], in_=o_sb[:, :last, :])
-        values(last)
-        for h in range(HALVES):
-            product(h, last)
-        nc.vector.tensor_copy(out=o_grouped[:, :P, :], in_=o_banks[0][:].rearrange("p t q -> p q t"))
-        nc.scalar.copy(out=o_grouped[:, P:, :], in_=o_banks[1][:].rearrange("p t q -> p q t"))
+            bank = sums.tile([P, PACK, P], F32, name="bank")
+            for t in range(PACK):
+                nc.tensor.matmul_mx(
+                    out=bank[:, t, :], lhsT=v_mx[t][0], lhsT_scale=v_mx[t][1],
+                    rhs=w_mx[h][0], rhs_scale=w_mx[h][1], start=True, stop=True,
+                )
+            o_sb = tile([P, PACK, P], F32, f"o_sb{h}")
+            if h == 0:
+                nc.scalar.copy(out=o_sb[:], in_=bank[:])
+                nc.sync.dma_start(out=out_rows[:, :, cols], in_=o_sb[:])
+                nc.vector.tensor_copy(out=o_grouped[:, cols, :], in_=bank[:].rearrange("p t q -> p q t"))
+            else:
+                nc.scalar.copy(out=o_grouped[:, cols, :], in_=bank[:].rearrange("p t q -> p q t"))
+                nc.scalar.copy(out=o_sb[:], in_=bank[:])
+                nc.scalar.dma_start(out=out_rows[:, :, cols], in_=o_sb[:])
         nc.vector.quantize_mx(
             out=o_codes[:].bitcast(FP8X4), scales=o_scales[:], in_=o_grouped[:].rearrange("p q t -> p (q t)")
         )
-        for h in range(HALVES):
-            nc.scalar.copy(out=o_sb[:, last, h * P : (h + 1) * P], in_=o_banks[h][:, last, :])
-        nc.scalar.dma_start(out=out_rows[:, last, :], in_=o_sb[:, last, :])
         nc.sync.dma_start(out=out_words, in_=o_codes[:].bitcast(I32))
         for quad in range(4):
-            queue = nc.sync if quad % 2 == 0 else nc.scalar
-            queue.dma_start(
+            nc.sync.dma_start(
                 out=out_2[0, 4 * quad : 4 * quad + 4, :].bitcast(I32),
                 in_=o_scales[32 * quad : 32 * quad + 4, :].bitcast(I32),
             )

@@ -109,21 +109,17 @@ def tile_attend_productkeys_pl_kernel(
                         out=bank[:], lhsT=q_codes[n][:, rows].bitcast(FP8X4), lhsT_scale=q_scales[n][:, rows],
                         rhs=keys, rhs_scale=book_scales[n][:, cols], start=True, stop=True,
                     )
-                    if (n, h, c) == (0, 0, 1):
-                        nc.vector.tensor_copy(out=whole[:, cols], in_=bank[:])
-                    else:
-                        nc.scalar.copy(out=whole[:, cols], in_=bank[:])
+                    nc.scalar.copy(out=whole[:, cols], in_=bank[:])
                 scores[n, h] = whole
 
         size_bank = spread.tile([P, PACK, P], F32, name="size_bank")
         for t in range(PACK):
             nc.tensor.transpose(size_bank[:, t, :], size_cols[:, t : t + 1].to_broadcast([P, P]), ident[:])
 
-        def turn(rows_bf16, grouped):
-            words = rows_bf16[:].bitcast(F32)
+        def turn(word_columns, grouped):
             turned = turns.tile([P, 2, P], F32, name="turned")
             for u in range(2):
-                nc.tensor.transpose(turned[:, u, :], words[:, u : I // 2 : 2], ident[:])
+                nc.tensor.transpose(turned[:, u, :], word_columns[u], ident[:])
             nc.scalar.copy(
                 out=grouped.bitcast(F32).rearrange("p (c u) -> p c u", u=2),
                 in_=turned[:].rearrange("p u c -> p c u"),
@@ -141,11 +137,12 @@ def tile_attend_productkeys_pl_kernel(
                 nc.scalar.activation(out=picked[:], in_=rounded[:].indirect(lists[2][:]), func=ACT.Copy)
             else:
                 nc.vector.tensor_copy(out=picked[:], in_=pool_rows[t][:].indirect(lists[2][:]))
-            turn(picked, early[:, t * I : (t + 1) * I] if t < PACK - 1 else v_last[:])
+            words = picked[:].bitcast(F32)
+            turn([words[:, u : I // 2 : 2] for u in range(2)], early[:, t * I : (t + 1) * I] if t < PACK - 1 else v_last[:])
 
         first = []
         for h in range(HALVES):
-            picked_b = tile([P, I], F32, f"picked_b{h}")
+            picked_b = tile([P, I], F32, f"picked_b{h}", tag="q_raw1" if h == 0 else None)
             nc.vector.tensor_copy(out=picked_b[:], in_=scores[0, h][:].indirect(lists[0][:]))
             first.append(picked_b)
 
@@ -170,12 +167,16 @@ def tile_attend_productkeys_pl_kernel(
         nc.vector.reciprocal(out=inv[:], in_=total[:])
 
         def weights(h, w, grouped):
-            nc.vector.scalar_tensor_tensor(
-                out=w[:].rearrange("p (s t) -> p s t", t=PACK),
-                in0=expd[h][:].rearrange("p (s t) -> p s t", t=PACK),
-                scalar=inv[:, h : h + 1], in1=size_bank[:].rearrange("p t s -> p s t"), op0=ALU.mult, op1=ALU.mult,
-            )
-            turn(w, grouped)
+            for u in range(2):
+                nc.vector.scalar_tensor_tensor(
+                    out=w[:, u * 2 * P : (u + 1) * 2 * P].rearrange("p (s e) -> p s e", e=2),
+                    in0=expd[h][:].rearrange("p (s t) -> p s t", t=PACK)[:, :, 2 * u : 2 * u + 2],
+                    scalar=inv[:, h : h + 1],
+                    in1=size_bank[:, 2 * u : 2 * u + 2, :].rearrange("p e s -> p s e"),
+                    op0=ALU.mult, op1=ALU.mult,
+                )
+            words = w[:].bitcast(F32)
+            turn([words[:, u * P : (u + 1) * P] for u in range(2)], grouped)
 
         weights(0, tile([P, I], BF16, "w0"), early[:, 3 * I :])
         values(PACK - 1)
@@ -200,27 +201,26 @@ def tile_attend_productkeys_pl_kernel(
         o_grouped = tile([P, Q, PACK], BF16, "o_grouped")
         for h in range(HALVES):
             cols = slice(h * P, (h + 1) * P)
-            bank = sums.tile([P, PACK, P], F32, name="bank")
-            for t in range(PACK):
-                nc.tensor.matmul_mx(
-                    out=bank[:, t, :], lhsT=v_mx[t][0], lhsT_scale=v_mx[t][1],
-                    rhs=w_mx[h][0], rhs_scale=w_mx[h][1], start=True, stop=True,
-                )
-            o_sb = tile([P, PACK, P], F32, f"o_sb{h}")
-            if h == 0:
+            for u in range(2):
+                bank = sums.tile([P, 2, P], F32, name="bank")
+                for e in range(2):
+                    nc.tensor.matmul_mx(
+                        out=bank[:, e, :], lhsT=v_mx[2 * u + e][0], lhsT_scale=v_mx[2 * u + e][1],
+                        rhs=w_mx[h][0], rhs_scale=w_mx[h][1], start=True, stop=True,
+                    )
+                places = slice(2 * u, 2 * u + 2)
+                o_sb = tile([P, 2, P], F32, f"o_sb{h}{u}")
+                nc.vector.tensor_copy(out=o_grouped[:, cols, places], in_=bank[:].rearrange("p e q -> p q e"))
                 nc.scalar.copy(out=o_sb[:], in_=bank[:])
-                nc.sync.dma_start(out=out_rows[:, :, cols], in_=o_sb[:])
-                nc.vector.tensor_copy(out=o_grouped[:, cols, :], in_=bank[:].rearrange("p t q -> p q t"))
-            else:
-                nc.scalar.copy(out=o_grouped[:, cols, :], in_=bank[:].rearrange("p t q -> p q t"))
-                nc.scalar.copy(out=o_sb[:], in_=bank[:])
-                nc.scalar.dma_start(out=out_rows[:, :, cols], in_=o_sb[:])
-        nc.vector.quantize_mx(
-            out=o_codes[:].bitcast(FP8X4), scales=o_scales[:], in_=o_grouped[:].rearrange("p q t -> p (q t)")
-        )
+                nc.sync.dma_start(out=out_rows[:, places, cols], in_=o_sb[:])
+            nc.vector.quantize_mx(
+                out=o_codes[:, cols].bitcast(FP8X4), scales=o_scales[:, cols],
+                in_=o_grouped[:, cols, :].rearrange("p q t -> p (q t)"),
+            )
         nc.sync.dma_start(out=out_words, in_=o_codes[:].bitcast(I32))
         for quad in range(4):
-            nc.sync.dma_start(
+            queue = nc.sync if quad % 2 == 0 else nc.scalar
+            queue.dma_start(
                 out=out_2[0, 4 * quad : 4 * quad + 4, :].bitcast(I32),
                 in_=o_scales[32 * quad : 32 * quad + 4, :].bitcast(I32),
             )

@@ -58,11 +58,11 @@ def tile_attend_productkeys_pl_kernel(
         nc.sync.dma_start(out=book1[:].bitcast(I32), in_=sub1_words[0].bitcast(I32))
         load_scales(nc.sync, book_scales[0], sub1_scales)
         nc.sync.dma_start(out=q_raw[1][:], in_=query2.rearrange("(p t) q -> p t q", t=PACK))
+        nc.sync.dma_start(lists[0][:], offs)
         nc.sync.dma_start(out=book2[:].bitcast(I32), in_=sub2_words[0].rearrange("p n t -> p (n t)").bitcast(I32))
         load_scales(nc.sync, book_scales[1], sub2_scales)
-        nc.sync.dma_start(lists[0][:], offs)
-        nc.sync.dma_start(out=pool_rows[0][:], in_=vals_by_place[0])
         nc.sync.dma_start(lists[1][:], offs2)
+        nc.sync.dma_start(out=pool_rows[0][:], in_=vals_by_place[0])
         nc.sync.dma_start(out=size_cols[:], in_=size.rearrange("o (p t) -> p (o t)", t=PACK))
         nc.sync.dma_start(lists[2][:], offs3)
         for t in range(1, PACK):
@@ -70,8 +70,6 @@ def tile_attend_productkeys_pl_kernel(
 
         ident = tile([P, P], F32, "ident")
         make_identity(nc, ident[:])
-        warm = tile([P, 1], F32, "warm")
-        nc.scalar.activation(out=warm[:], in_=ident[:, 0:1], func=ACT.Exp)
 
         q_codes, q_scales = [], []
         for n in range(2):
@@ -80,7 +78,8 @@ def tile_attend_productkeys_pl_kernel(
             scales = tile([P, Q], U8, f"q_scales{n}")
             for h in range(HALVES):
                 rows = slice(h * P, (h + 1) * P)
-                nc.vector.tensor_copy(
+                cast = nc.scalar.copy if (n, h) == (0, 1) else nc.vector.tensor_copy
+                cast(
                     out=grouped[:, rows, :].rearrange("p (c i) t -> p c t i", i=4),
                     in_=q_raw[n][:, :, rows].rearrange("p t (c i) -> p c t i", i=4),
                 )
@@ -129,15 +128,19 @@ def tile_attend_productkeys_pl_kernel(
         v_last = tile([P, I], BF16, "v_last")
         w_last = tile([P, I], BF16, "w_last")
 
-        def values(t):
-            picked = tile([P, I], BF16, f"picked{t}")
+        picked_all = [tile([P, I], BF16, f"picked{t}") for t in range(PACK)]
+
+        def gather_values(t):
+            picked = picked_all[t]
             if t == 0:
                 rounded = tile([P, T], BF16, "rounded")
                 nc.scalar.activation(out=rounded[:], in_=pool_rows[t][:], func=ACT.Copy)
                 nc.scalar.activation(out=picked[:], in_=rounded[:].indirect(lists[2][:]), func=ACT.Copy)
             else:
                 nc.vector.tensor_copy(out=picked[:], in_=pool_rows[t][:].indirect(lists[2][:]))
-            words = picked[:].bitcast(F32)
+
+        def turn_values(t):
+            words = picked_all[t][:].bitcast(F32)
             turn([words[:, u : I // 2 : 2] for u in range(2)], early[:, t * I : (t + 1) * I] if t < PACK - 1 else v_last[:])
 
         first = []
@@ -154,34 +157,42 @@ def tile_attend_productkeys_pl_kernel(
         neg_max = tile([P, HALVES], F32, "neg_max")
         nc.vector.tensor_reduce(out=neg_max[:], in_=logits[:], axis=AXIS.X, op=ALU.max, negate=True)
 
-        for t in range(PACK - 1):
-            values(t)
-        expd = [tile([P, I], F32, "expd0", tag="rounded"), tile([P, I], F32, "expd1")]
-        total = tile([P, HALVES], F32, "total")
+        gather_values(0)
+        gather_values(1)
+        expd_all = tile([P, HALVES, I], F32, "expd", tag="rounded")
+        expd = [expd_all[:, h, :] for h in range(HALVES)]
+        total = [tile([P, 1], F32, f"total{h}") for h in range(HALVES)]
+        after_v2 = tile([P, I // 2 + 16], F32, "after_v2", tag="pool_rows2")
+        inv = [tile([P, 1], F32, "inv0")[:], after_v2[:, I // 2 : I // 2 + 1]]
         for h in range(HALVES):
             nc.scalar.activation(
-                out=expd[h][:], in_=logits[:, h, :], func=ACT.Exp, bias=neg_max[:, h : h + 1], scale=1.0,
-                accum_out=total[:, h : h + 1],
+                out=expd[h], in_=logits[:, h, :], func=ACT.Exp, bias=neg_max[:, h : h + 1], scale=1.0,
+                accum_out=total[h][:],
             )
-        inv = tile([P, HALVES], F32, "inv", tag="pool_rows2")
-        nc.vector.reciprocal(out=inv[:], in_=total[:])
+        turn_values(0)
+        turn_values(1)
+        nc.vector.reciprocal(out=inv[0], in_=total[0][:])
+        gather_values(2)
+        turn_values(2)
+        nc.vector.reciprocal(out=inv[1], in_=total[1][:])
 
         def weights(h, w, grouped):
             for u in range(2):
                 nc.vector.scalar_tensor_tensor(
                     out=w[:, u * 2 * P : (u + 1) * 2 * P].rearrange("p (s e) -> p s e", e=2),
-                    in0=expd[h][:].rearrange("p (s t) -> p s t", t=PACK)[:, :, 2 * u : 2 * u + 2],
-                    scalar=inv[:, h : h + 1],
+                    in0=expd[h].rearrange("p (s t) -> p s t", t=PACK)[:, :, 2 * u : 2 * u + 2],
+                    scalar=inv[h],
                     in1=size_bank[:, 2 * u : 2 * u + 2, :].rearrange("p e s -> p s e"),
                     op0=ALU.mult, op1=ALU.mult,
                 )
-            words = w[:].bitcast(F32)
+            words = w.bitcast(F32)
             turn([words[:, u * P : (u + 1) * P] for u in range(2)], grouped)
 
-        weights(0, tile([P, I], BF16, "w0"), early[:, 3 * I :])
-        values(PACK - 1)
+        weights(0, after_v2[:, : I // 2].bitcast(BF16), early[:, 3 * I :])
+        gather_values(PACK - 1)
+        turn_values(PACK - 1)
         w1 = tile([P, I], BF16, "w1", tag="pool_rows3")
-        weights(1, w1, w_last[:])
+        weights(1, w1[:], w_last[:])
 
         def quantise(grouped, name, tag=None):
             width = grouped.shape[1] // PACK
@@ -190,7 +201,7 @@ def tile_attend_productkeys_pl_kernel(
             nc.vector.quantize_mx(out=codes[:].bitcast(FP8X4), scales=scales[:], in_=grouped[:])
             return [(codes[:, c : c + P].bitcast(FP8X4), scales[:, c : c + P]) for c in range(0, width, P)]
 
-        early_mx = quantise(early, "early", tag="expd1")
+        early_mx = quantise(early, "early", tag="rounded")
         v_mx = early_mx[:3] + quantise(v_last, "v_last")
         w_mx = early_mx[3:] + quantise(w_last, "w_last")
 
@@ -201,6 +212,7 @@ def tile_attend_productkeys_pl_kernel(
         o_grouped = tile([P, Q, PACK], BF16, "o_grouped")
         for h in range(HALVES):
             cols = slice(h * P, (h + 1) * P)
+            o_sb = tile([P, PACK, P], F32, f"o_sb{h}")
             for u in range(2):
                 bank = sums.tile([P, 2, P], F32, name="bank")
                 for e in range(2):
@@ -209,14 +221,18 @@ def tile_attend_productkeys_pl_kernel(
                         rhs=w_mx[h][0], rhs_scale=w_mx[h][1], start=True, stop=True,
                     )
                 places = slice(2 * u, 2 * u + 2)
-                o_sb = tile([P, 2, P], F32, f"o_sb{h}{u}")
-                nc.vector.tensor_copy(out=o_grouped[:, cols, places], in_=bank[:].rearrange("p e q -> p q e"))
-                nc.scalar.copy(out=o_sb[:], in_=bank[:])
-                nc.sync.dma_start(out=out_rows[:, places, cols], in_=o_sb[:])
-            nc.vector.quantize_mx(
-                out=o_codes[:, cols].bitcast(FP8X4), scales=o_scales[:, cols],
-                in_=o_grouped[:, cols, :].rearrange("p q t -> p (q t)"),
+                nc.scalar.copy(out=o_sb[:, places, :], in_=bank[:])
+                if h == 1:
+                    nc.sync.dma_start(out=out_rows[:, places, cols], in_=o_sb[:, places, :])
+            if h == 0:
+                nc.sync.dma_start(out=out_rows[:, :, cols], in_=o_sb[:])
+            nc.vector.tensor_copy(
+                out=o_grouped[:, cols, :].rearrange("p (c i) t -> p c t i", i=4),
+                in_=o_sb[:].rearrange("p t (c i) -> p c t i", i=4),
             )
+        nc.vector.quantize_mx(
+            out=o_codes[:].bitcast(FP8X4), scales=o_scales[:], in_=o_grouped[:].rearrange("p q t -> p (q t)"),
+        )
         nc.sync.dma_start(out=out_words, in_=o_codes[:].bitcast(I32))
         for quad in range(4):
             queue = nc.sync if quad % 2 == 0 else nc.scalar

@@ -31,42 +31,47 @@ def tile_attend_productkeys_pl_kernel(
     nc = tc.nc
     with ExitStack() as ctx:
         keep = ctx.enter_context(tc.tile_pool(name="keep", bufs=1))
+        shared = ctx.enter_context(tc.tile_pool(name="shared", bufs=1))
         sums = ctx.enter_context(tc.psum_pool(name="sums", bufs=4))
-        turns = ctx.enter_context(tc.psum_pool(name="turns", bufs=3))
-        spread = ctx.enter_context(tc.psum_pool(name="spread", bufs=1))
+        turns = ctx.enter_context(tc.psum_pool(name="turns", bufs=2))
+        turned_weights = ctx.enter_context(tc.psum_pool(name="turned_weights", bufs=2))
 
         def tile(shape, dtype, name, tag=None):
             return keep.tile(shape, dtype, name=name, tag=tag or name, align_bytes=64)
+
+        def on_last_values(shape, dtype, name, offset):
+            return shared.tile(shape, dtype, name=name, offset=offset, align_bytes=64)
 
         q_raw = [tile([P, PACK, Q], F32, f"q_raw{n}") for n in range(2)]
         book1 = tile([P, 2 * U], U8, "book1")
         book2 = tile([P, V], U32, "book2")
         book_scales = [tile([P, U], U8, f"book_scales{n}") for n in range(2)]
         lists = [keep.tile([P, I // 16], U16, name=f"list{n}") for n in range(3)]
-        pool_rows = [tile([P, T], F32, f"pool_rows{t}") for t in range(PACK)]
+        pool_rows = [tile([P, T], F32, f"pool_rows{t}") for t in range(PACK - 1)]
+        pool_rows.append(on_last_values([P, T], F32, "pool_rows3", 0))
         size_cols = tile([P, PACK], F32, "size_cols")
         vals_by_place = vals.rearrange("(p t) n -> t p n", t=PACK)
 
-        def load_scales(queue, plane, rows):
+        def load_scales(plane, rows):
             for quad in range(4):
-                queue.dma_start(
+                nc.sync.dma_start(
                     out=plane[32 * quad : 32 * quad + 4, :].bitcast(I32),
                     in_=rows[0, 4 * quad : 4 * quad + 4, :].bitcast(I32),
                 )
 
         nc.sync.dma_start(out=q_raw[0][:], in_=query.rearrange("(p t) q -> p t q", t=PACK))
         nc.sync.dma_start(out=book1[:].bitcast(I32), in_=sub1_words[0].bitcast(I32))
-        load_scales(nc.sync, book_scales[0], sub1_scales)
+        load_scales(book_scales[0], sub1_scales)
         nc.sync.dma_start(out=q_raw[1][:], in_=query2.rearrange("(p t) q -> p t q", t=PACK))
         nc.sync.dma_start(lists[0][:], offs)
         nc.sync.dma_start(out=book2[:].bitcast(I32), in_=sub2_words[0].rearrange("p n t -> p (n t)").bitcast(I32))
-        load_scales(nc.sync, book_scales[1], sub2_scales)
+        load_scales(book_scales[1], sub2_scales)
         nc.sync.dma_start(lists[1][:], offs2)
         nc.sync.dma_start(out=pool_rows[0][:], in_=vals_by_place[0])
-        nc.sync.dma_start(out=size_cols[:], in_=size.rearrange("o (p t) -> p (o t)", t=PACK))
         nc.sync.dma_start(lists[2][:], offs3)
         for t in range(1, PACK):
             nc.sync.dma_start(out=pool_rows[t][:], in_=vals_by_place[t])
+        nc.sync.dma_start(out=size_cols[:], in_=size.rearrange("o (p t) -> p (o t)", t=PACK))
 
         ident = tile([P, P], F32, "ident")
         make_identity(nc, ident[:])
@@ -111,37 +116,27 @@ def tile_attend_productkeys_pl_kernel(
                     nc.scalar.copy(out=whole[:, cols], in_=bank[:])
                 scores[n, h] = whole
 
-        size_bank = spread.tile([P, PACK, P], F32, name="size_bank")
-        for t in range(PACK):
-            nc.tensor.transpose(size_bank[:, t, :], size_cols[:, t : t + 1].to_broadcast([P, P]), ident[:])
+        picked = [tile([P, I], BF16, f"picked{t}") for t in range(PACK)]
 
-        def turn(word_columns, grouped):
+        def turn_values(t, grouped):
+            words = picked[t][:].bitcast(F32)
             turned = turns.tile([P, 2, P], F32, name="turned")
             for u in range(2):
-                nc.tensor.transpose(turned[:, u, :], word_columns[u], ident[:])
+                nc.tensor.transpose(turned[:, u, :], words[:, u : I // 2 : 2], ident[:])
             nc.scalar.copy(
                 out=grouped.bitcast(F32).rearrange("p (c u) -> p c u", u=2),
                 in_=turned[:].rearrange("p u c -> p c u"),
             )
 
-        early = tile([P, 4 * I], BF16, "early")
-        v_last = tile([P, I], BF16, "v_last")
-        w_last = tile([P, I], BF16, "w_last")
+        def quantise(grouped, name, codes):
+            width = grouped.shape[1] // PACK
+            scales = tile([P, width], U8, name + "_scales")
+            nc.vector.quantize_mx(out=codes[:].bitcast(FP8X4), scales=scales[:], in_=grouped)
+            return [(codes[:, c : c + P].bitcast(FP8X4), scales[:, c : c + P]) for c in range(0, width, P)]
 
-        picked_all = [tile([P, I], BF16, f"picked{t}") for t in range(PACK)]
-
-        def gather_values(t):
-            picked = picked_all[t]
-            if t == 0:
-                rounded = tile([P, T], BF16, "rounded")
-                nc.scalar.activation(out=rounded[:], in_=pool_rows[t][:], func=ACT.Copy)
-                nc.scalar.activation(out=picked[:], in_=rounded[:].indirect(lists[2][:]), func=ACT.Copy)
-            else:
-                nc.vector.tensor_copy(out=picked[:], in_=pool_rows[t][:].indirect(lists[2][:]))
-
-        def turn_values(t):
-            words = picked_all[t][:].bitcast(F32)
-            turn([words[:, u : I // 2 : 2] for u in range(2)], early[:, t * I : (t + 1) * I] if t < PACK - 1 else v_last[:])
+        rounded = tile([P, T], BF16, "rounded")
+        nc.scalar.activation(out=rounded[:], in_=pool_rows[0][:], func=ACT.Copy)
+        nc.scalar.activation(out=picked[0][:], in_=rounded[:].indirect(lists[2][:]), func=ACT.Copy)
 
         first = []
         for h in range(HALVES):
@@ -157,53 +152,50 @@ def tile_attend_productkeys_pl_kernel(
         neg_max = tile([P, HALVES], F32, "neg_max")
         nc.vector.tensor_reduce(out=neg_max[:], in_=logits[:], axis=AXIS.X, op=ALU.max, negate=True)
 
-        gather_values(0)
-        gather_values(1)
-        expd_all = tile([P, HALVES, I], F32, "expd", tag="rounded")
-        expd = [expd_all[:, h, :] for h in range(HALVES)]
-        total = [tile([P, 1], F32, f"total{h}") for h in range(HALVES)]
-        after_v2 = tile([P, I // 2 + 16], F32, "after_v2", tag="pool_rows2")
-        inv = [tile([P, 1], F32, "inv0")[:], after_v2[:, I // 2 : I // 2 + 1]]
+        expd = tile([P, HALVES, I], F32, "expd", tag="rounded")
+        total = tile([P, HALVES], F32, "total")
         for h in range(HALVES):
             nc.scalar.activation(
-                out=expd[h], in_=logits[:, h, :], func=ACT.Exp, bias=neg_max[:, h : h + 1], scale=1.0,
-                accum_out=total[h][:],
+                out=expd[:, h, :], in_=logits[:, h, :], func=ACT.Exp, bias=neg_max[:, h : h + 1], scale=1.0,
+                accum_out=total[:, h : h + 1],
             )
-        turn_values(0)
-        turn_values(1)
-        nc.vector.reciprocal(out=inv[0], in_=total[0][:])
-        gather_values(2)
-        turn_values(2)
-        nc.vector.reciprocal(out=inv[1], in_=total[1][:])
+        for t in (1, 2):
+            nc.vector.tensor_copy(out=picked[t][:], in_=pool_rows[t][:].indirect(lists[2][:]))
+        inv = tile([P, HALVES], F32, "inv", tag="pool_rows2")
+        nc.vector.reciprocal(out=inv[:], in_=total[:])
+        nc.vector.tensor_copy(out=picked[3][:], in_=pool_rows[3][:].indirect(lists[2][:]))
 
-        def weights(h, w, grouped):
-            for u in range(2):
-                nc.vector.scalar_tensor_tensor(
-                    out=w[:, u * 2 * P : (u + 1) * 2 * P].rearrange("p (s e) -> p s e", e=2),
-                    in0=expd[h].rearrange("p (s t) -> p s t", t=PACK)[:, :, 2 * u : 2 * u + 2],
-                    scalar=inv[h],
-                    in1=size_bank[:, 2 * u : 2 * u + 2, :].rearrange("p e s -> p s e"),
-                    op0=ALU.mult, op1=ALU.mult,
-                )
-            words = w.bitcast(F32)
-            turn([words[:, u * P : (u + 1) * P] for u in range(2)], grouped)
+        v_first = tile([P, 2 * I], BF16, "v_first", tag="logits")
+        for t in (0, 1):
+            turn_values(t, v_first[:, t * I : (t + 1) * I])
 
-        weights(0, after_v2[:, : I // 2].bitcast(BF16), early[:, 3 * I :])
-        gather_values(PACK - 1)
-        turn_values(PACK - 1)
-        w1 = tile([P, I], BF16, "w1", tag="pool_rows3")
-        weights(1, w1[:], w_last[:])
+        w_turned = []
+        for h in range(HALVES):
+            shares = tile([P, PACK, P], F32, f"shares{h}")
+            nc.scalar.activation(
+                out=shares[:].rearrange("p t (c i) -> p c t i", i=4),
+                in_=expd[:, h, :].rearrange("p (c i t) -> p c t i", i=4, t=PACK),
+                func=ACT.Copy, scale=inv[:, h : h + 1],
+            )
+            turned = turned_weights.tile([P, PACK, P], F32, name="turned_w")
+            for t in range(PACK):
+                nc.tensor.transpose(turned[:, t, :], shares[:, t, :], ident[:])
+            w_turned.append(turned)
 
-        def quantise(grouped, name, tag=None):
-            width = grouped.shape[1] // PACK
-            codes = tile([P, width], U32, name + "_codes", tag=tag)
-            scales = tile([P, width], U8, name + "_scales")
-            nc.vector.quantize_mx(out=codes[:].bitcast(FP8X4), scales=scales[:], in_=grouped[:])
-            return [(codes[:, c : c + P].bitcast(FP8X4), scales[:, c : c + P]) for c in range(0, width, P)]
+        v_second = tile([P, 2 * I], BF16, "v_second", tag="rounded")
+        for t in (2, 3):
+            turn_values(t, v_second[:, (t - 2) * I : (t - 1) * I])
 
-        early_mx = quantise(early, "early", tag="rounded")
-        v_mx = early_mx[:3] + quantise(v_last, "v_last")
-        w_mx = early_mx[3:] + quantise(w_last, "w_last")
+        v_mx = quantise(v_first[:], "v_first", on_last_values([P, 2 * P], U32, "v_first_codes", 0))
+        w_grouped = on_last_values([P, HALVES, P, PACK], BF16, "w_grouped", 1024)
+        for h in range(HALVES):
+            nc.vector.tensor_tensor(
+                out=w_grouped[:, h, :, :], in0=w_turned[h][:].rearrange("p t q -> p q t"),
+                in1=size_cols[:].unsqueeze(1).to_broadcast([P, P, PACK]), op=ALU.mult,
+            )
+        w_mx = quantise(w_grouped[:, 0, :, :].rearrange("p q t -> p (q t)"), "w0", tile([P, P], U32, "w0_codes"))
+        v_mx = v_mx + quantise(v_second[:], "v_second", tile([P, 2 * P], U32, "v_second_codes"))
+        w_mx = w_mx + quantise(w_grouped[:, 1, :, :].rearrange("p q t -> p (q t)"), "w1", tile([P, P], U32, "w1_codes"))
 
         o_codes = tile([P, Q], U32, "o_codes")
         o_scales = tile([P, Q], U8, "o_scales")

@@ -33,8 +33,7 @@ def tile_attend_productkeys_pl_kernel(
         keep = ctx.enter_context(tc.tile_pool(name="keep", bufs=1))
         shared = ctx.enter_context(tc.tile_pool(name="shared", bufs=1))
         sums = ctx.enter_context(tc.psum_pool(name="sums", bufs=4))
-        turns = ctx.enter_context(tc.psum_pool(name="turns", bufs=2))
-        turned_weights = ctx.enter_context(tc.psum_pool(name="turned_weights", bufs=2))
+        turns = ctx.enter_context(tc.psum_pool(name="turns", bufs=4))
 
         def tile(shape, dtype, name, tag=None):
             return keep.tile(shape, dtype, name=name, tag=tag or name, align_bytes=64)
@@ -75,6 +74,8 @@ def tile_attend_productkeys_pl_kernel(
 
         ident = tile([P, P], F32, "ident")
         make_identity(nc, ident[:])
+        minus_one = tile([P, 1], F32, "minus_one")
+        nc.gpsimd.memset(minus_one[:], -1.0)
 
         q_codes, q_scales = [], []
         for n in range(2):
@@ -161,13 +162,10 @@ def tile_attend_productkeys_pl_kernel(
             )
         for t in (1, 2):
             nc.vector.tensor_copy(out=picked[t][:], in_=pool_rows[t][:].indirect(lists[2][:]))
-        inv = tile([P, HALVES], F32, "inv", tag="pool_rows2")
-        nc.vector.reciprocal(out=inv[:], in_=total[:])
+        inv = tile([P, HALVES], F32, "inv")
+        for h in range(HALVES):
+            nc.gpsimd.tensor_tensor(out=inv[:, h : h + 1], in0=total[:, h : h + 1], in1=minus_one[:], op=ALU.pow)
         nc.vector.tensor_copy(out=picked[3][:], in_=pool_rows[3][:].indirect(lists[2][:]))
-
-        v_first = tile([P, 2 * I], BF16, "v_first", tag="logits")
-        for t in (0, 1):
-            turn_values(t, v_first[:, t * I : (t + 1) * I])
 
         w_turned = []
         for h in range(HALVES):
@@ -177,24 +175,24 @@ def tile_attend_productkeys_pl_kernel(
                 in_=expd[:, h, :].rearrange("p (c i t) -> p c t i", i=4, t=PACK),
                 func=ACT.Copy, scale=inv[:, h : h + 1],
             )
-            turned = turned_weights.tile([P, PACK, P], F32, name="turned_w")
+            turned = sums.tile([P, PACK, P], F32, name="bank")
             for t in range(PACK):
                 nc.tensor.transpose(turned[:, t, :], shares[:, t, :], ident[:])
             w_turned.append(turned)
 
-        v_second = tile([P, 2 * I], BF16, "v_second", tag="rounded")
-        for t in (2, 3):
-            turn_values(t, v_second[:, (t - 2) * I : (t - 1) * I])
+        v_grouped = tile([P, PACK * I], BF16, "v_grouped", tag="rounded")
+        for t in range(PACK):
+            turn_values(t, v_grouped[:, t * I : (t + 1) * I])
 
-        v_mx = quantise(v_first[:], "v_first", on_last_values([P, 2 * P], U32, "v_first_codes", 0))
         w_grouped = on_last_values([P, HALVES, P, PACK], BF16, "w_grouped", 1024)
         for h in range(HALVES):
             nc.vector.tensor_tensor(
                 out=w_grouped[:, h, :, :], in0=w_turned[h][:].rearrange("p t q -> p q t"),
                 in1=size_cols[:].unsqueeze(1).to_broadcast([P, P, PACK]), op=ALU.mult,
             )
+        v_mx = quantise(v_grouped[:, : 2 * I], "v_first", on_last_values([P, 2 * P], U32, "v_first_codes", 0))
         w_mx = quantise(w_grouped[:, 0, :, :].rearrange("p q t -> p (q t)"), "w0", tile([P, P], U32, "w0_codes"))
-        v_mx = v_mx + quantise(v_second[:], "v_second", tile([P, 2 * P], U32, "v_second_codes"))
+        v_mx = v_mx + quantise(v_grouped[:, 2 * I :], "v_second", tile([P, 2 * P], U32, "v_second_codes"))
         w_mx = w_mx + quantise(w_grouped[:, 1, :, :].rearrange("p q t -> p (q t)"), "w1", tile([P, P], U32, "w1_codes"))
 
         o_codes = tile([P, Q], U32, "o_codes")

@@ -62,14 +62,15 @@ def tile_attend_productkeys_pl_kernel(
         nc.sync.dma_start(out=book1[:].bitcast(I32), in_=sub1_words[0].bitcast(I32))
         load_scales(book_scales[0], sub1_scales)
         nc.sync.dma_start(out=q_raw[1][:], in_=query2.rearrange("(p t) q -> p t q", t=PACK))
-        nc.sync.dma_start(lists[0][:], offs)
         nc.sync.dma_start(out=book2[:].bitcast(I32), in_=sub2_words[0].rearrange("p n t -> p (n t)").bitcast(I32))
+        nc.sync.dma_start(lists[0][:], offs)
         load_scales(book_scales[1], sub2_scales)
-        nc.sync.dma_start(lists[1][:], offs2)
         nc.sync.dma_start(out=pool_rows[0][:], in_=vals_by_place[0])
+        nc.sync.dma_start(lists[1][:], offs2)
         nc.sync.dma_start(lists[2][:], offs3)
-        for t in range(1, PACK):
-            nc.sync.dma_start(out=pool_rows[t][:], in_=vals_by_place[t])
+        nc.sync.dma_start(out=pool_rows[1][:], in_=vals_by_place[1])
+        nc.sync.dma_start(out=pool_rows[2][:], in_=vals_by_place[2])
+        nc.sync.dma_start(out=pool_rows[3][:], in_=vals_by_place[3])
         nc.sync.dma_start(out=size_cols[:], in_=size.rearrange("o (p t) -> p (o t)", t=PACK))
 
         ident = tile([P, P], F32, "ident")

@@ -22,6 +22,7 @@ P = 128
 PACK = 4
 BANK = 512
 HALVES = Q // P
+CAST_SHARE = 1024
 
 
 def tile_attend_productkeys_pl_kernel(
@@ -48,7 +49,7 @@ def tile_attend_productkeys_pl_kernel(
         lists = [keep.tile([P, I // 16], U16, name=f"list{n}") for n in range(3)]
         pool_rows = [tile([P, T], F32, f"pool_rows{t}") for t in range(PACK - 1)]
         pool_rows.append(on_last_values([P, T], F32, "pool_rows3", 0))
-        size_cols = tile([P, PACK], F32, "size_cols")
+        size_cols = on_last_values([P, PACK], F32, "size_cols", 4 * T)
         vals_by_place = vals.rearrange("(p t) n -> t p n", t=PACK)
 
         def load_scales(plane, rows):
@@ -137,7 +138,8 @@ def tile_attend_productkeys_pl_kernel(
             return [(codes[:, c : c + P].bitcast(FP8X4), scales[:, c : c + P]) for c in range(0, width, P)]
 
         rounded = tile([P, T], BF16, "rounded")
-        nc.scalar.activation(out=rounded[:], in_=pool_rows[0][:], func=ACT.Copy)
+        nc.vector.tensor_copy(out=rounded[:, :CAST_SHARE], in_=pool_rows[0][:, :CAST_SHARE])
+        nc.scalar.activation(out=rounded[:, CAST_SHARE:], in_=pool_rows[0][:, CAST_SHARE:], func=ACT.Copy)
         nc.scalar.activation(out=picked[0][:], in_=rounded[:].indirect(lists[2][:]), func=ACT.Copy)
 
         first = []
@@ -152,7 +154,10 @@ def tile_attend_productkeys_pl_kernel(
                 out=logits[:, h, :], in0=scores[1, h][:].indirect(lists[1][:]), in1=first[h][:], op=ALU.add
             )
         neg_max = tile([P, HALVES], F32, "neg_max")
-        nc.vector.tensor_reduce(out=neg_max[:], in_=logits[:], axis=AXIS.X, op=ALU.max, negate=True)
+        for h in range(HALVES):
+            nc.vector.tensor_reduce(
+                out=neg_max[:, h : h + 1], in_=logits[:, h, :], axis=AXIS.X, op=ALU.max, negate=True
+            )
 
         expd = tile([P, HALVES, I], F32, "expd", tag="rounded")
         total = tile([P, HALVES], F32, "total")
@@ -185,7 +190,7 @@ def tile_attend_productkeys_pl_kernel(
         for t in range(PACK):
             turn_values(t, v_grouped[:, t * I : (t + 1) * I])
 
-        w_grouped = on_last_values([P, HALVES, P, PACK], BF16, "w_grouped", 1024)
+        w_grouped = tile([P, HALVES, P, PACK], BF16, "w_grouped")
         for h in range(HALVES):
             nc.vector.tensor_tensor(
                 out=w_grouped[:, h, :, :], in0=w_turned[h][:].rearrange("p t q -> p q t"),
@@ -193,7 +198,7 @@ def tile_attend_productkeys_pl_kernel(
             )
         v_mx = quantise(v_grouped[:, : 2 * I], "v_first", on_last_values([P, 2 * P], U32, "v_first_codes", 0))
         w_mx = quantise(w_grouped[:, 0, :, :].rearrange("p q t -> p (q t)"), "w0", tile([P, P], U32, "w0_codes"))
-        v_mx = v_mx + quantise(v_grouped[:, 2 * I :], "v_second", tile([P, 2 * P], U32, "v_second_codes"))
+        v_mx = v_mx + quantise(v_grouped[:, 2 * I :], "v_second", on_last_values([P, 2 * P], U32, "v_second_codes", 4 * T))
         w_mx = w_mx + quantise(w_grouped[:, 1, :, :].rearrange("p q t -> p (q t)"), "w1", tile([P, P], U32, "w1_codes"))
 
         o_codes = tile([P, Q], U32, "o_codes")

@@ -134,7 +134,7 @@ def tile_attend_productkeys_pl_kernel(
         def quantise(grouped, name, codes):
             width = grouped.shape[1] // PACK
             scales = tile([P, width], U8, name + "_scales")
-            nc.vector.quantize_mx(out=codes[:].bitcast(FP8X4), scales=scales[:], in_=grouped)
+            nc.vector.quantize_mx(out=codes[:, :].bitcast(FP8X4), scales=scales[:], in_=grouped)
             return [(codes[:, c : c + P].bitcast(FP8X4), scales[:, c : c + P]) for c in range(0, width, P)]
 
         rounded = tile([P, T], BF16, "rounded")
@@ -196,9 +196,10 @@ def tile_attend_productkeys_pl_kernel(
                 out=w_grouped[:, h, :, :], in0=w_turned[h][:].rearrange("p t q -> p q t"),
                 in1=size_cols[:].unsqueeze(1).to_broadcast([P, P, PACK]), op=ALU.mult,
             )
-        v_mx = quantise(v_grouped[:, : 2 * I], "v_first", on_last_values([P, 2 * P], U32, "v_first_codes", 0))
         w_mx = quantise(w_grouped[:, 0, :, :].rearrange("p q t -> p (q t)"), "w0", tile([P, P], U32, "w0_codes"))
-        v_mx = v_mx + quantise(v_grouped[:, 2 * I :], "v_second", on_last_values([P, 2 * P], U32, "v_second_codes", 4 * T))
+        v_codes = on_last_values([P, PACK * P], U32, "v_codes", 4 * T)
+        v_mx = quantise(v_grouped[:, : 2 * I], "v_first", v_codes[:, : 2 * P])
+        v_mx = v_mx + quantise(v_grouped[:, 2 * I :], "v_second", v_codes[:, 2 * P :])
         w_mx = w_mx + quantise(w_grouped[:, 1, :, :].rearrange("p q t -> p (q t)"), "w1", tile([P, P], U32, "w1_codes"))
 
         o_codes = tile([P, Q], U32, "o_codes")

@@ -210,6 +210,14 @@ def tile_attend_productkeys_pl_kernel(
         for h in range(HALVES):
             cols = slice(h * P, (h + 1) * P)
             o_sb = tile([P, PACK, P], F32, f"o_sb{h}")
+            if h == 1:
+                whole_bank = turns.tile([P, PACK, P], F32, name="turned")
+                for t in range(PACK):
+                    nc.tensor.matmul_mx(
+                        out=whole_bank[:, t, :], lhsT=v_mx[t][0], lhsT_scale=v_mx[t][1],
+                        rhs=w_mx[h][0], rhs_scale=w_mx[h][1], start=True, stop=True,
+                    )
+                nc.vector.tensor_copy(out=o_grouped[:, cols, :], in_=whole_bank[:].rearrange("p t q -> p q t"))
             for u in range(2):
                 bank = sums.tile([P, 2, P], F32, name="bank")
                 for e in range(2):
@@ -223,13 +231,17 @@ def tile_attend_productkeys_pl_kernel(
                     nc.sync.dma_start(out=out_rows[:, places, cols], in_=o_sb[:, places, :])
             if h == 0:
                 nc.sync.dma_start(out=out_rows[:, :, cols], in_=o_sb[:])
-            nc.vector.tensor_copy(
-                out=o_grouped[:, cols, :].rearrange("p (c i) t -> p c t i", i=4),
-                in_=o_sb[:].rearrange("p t (c i) -> p c t i", i=4),
+            if h == 0:
+                nc.vector.tensor_copy(
+                    out=o_grouped[:, cols, :].rearrange("p (c i) t -> p c t i", i=4),
+                    in_=o_sb[:].rearrange("p t (c i) -> p c t i", i=4),
+                )
+        for h in range(HALVES):
+            cols = slice(h * P, (h + 1) * P)
+            nc.vector.quantize_mx(
+                out=o_codes[:, cols].bitcast(FP8X4), scales=o_scales[:, cols],
+                in_=o_grouped[:, cols, :].rearrange("p q t -> p (q t)"),
             )
-        nc.vector.quantize_mx(
-            out=o_codes[:].bitcast(FP8X4), scales=o_scales[:], in_=o_grouped[:].rearrange("p q t -> p (q t)"),
-        )
         nc.sync.dma_start(out=out_words, in_=o_codes[:].bitcast(I32))
         for quad in range(4):
             queue = nc.sync if quad % 2 == 0 else nc.scalar

@@ -22,7 +22,6 @@ P = 128
 PACK = 4
 BANK = 512
 HALVES = Q // P
-CAST_SHARE = 1024
 
 
 def tile_attend_productkeys_pl_kernel(
@@ -137,10 +136,8 @@ def tile_attend_productkeys_pl_kernel(
             nc.vector.quantize_mx(out=codes[:, :].bitcast(FP8X4), scales=scales[:], in_=grouped)
             return [(codes[:, c : c + P].bitcast(FP8X4), scales[:, c : c + P]) for c in range(0, width, P)]
 
-        rounded = tile([P, T], BF16, "rounded")
-        nc.vector.tensor_copy(out=rounded[:, :CAST_SHARE], in_=pool_rows[0][:, :CAST_SHARE])
-        nc.scalar.activation(out=rounded[:, CAST_SHARE:], in_=pool_rows[0][:, CAST_SHARE:], func=ACT.Copy)
-        nc.scalar.activation(out=picked[0][:], in_=rounded[:].indirect(lists[2][:]), func=ACT.Copy)
+        for t in (0, 1):
+            nc.scalar.activation(out=picked[t][:], in_=pool_rows[t][:].indirect(lists[2][:]), func=ACT.Copy)
 
         first = []
         for h in range(HALVES):
@@ -159,15 +156,14 @@ def tile_attend_productkeys_pl_kernel(
                 out=neg_max[:, h : h + 1], in_=logits[:, h, :], axis=AXIS.X, op=ALU.max, negate=True
             )
 
-        expd = tile([P, HALVES, I], F32, "expd", tag="rounded")
+        expd = tile([P, HALVES, I], F32, "expd", tag="pool_rows1")
         total = tile([P, HALVES], F32, "total")
         for h in range(HALVES):
             nc.scalar.activation(
                 out=expd[:, h, :], in_=logits[:, h, :], func=ACT.Exp, bias=neg_max[:, h : h + 1], scale=1.0,
                 accum_out=total[:, h : h + 1],
             )
-        for t in (1, 2):
-            nc.vector.tensor_copy(out=picked[t][:], in_=pool_rows[t][:].indirect(lists[2][:]))
+        nc.vector.tensor_copy(out=picked[2][:], in_=pool_rows[2][:].indirect(lists[2][:]))
         inv = tile([P, HALVES], F32, "inv")
         for h in range(HALVES):
             nc.gpsimd.tensor_tensor(out=inv[:, h : h + 1], in0=total[:, h : h + 1], in1=minus_one[:], op=ALU.pow)
@@ -186,7 +182,7 @@ def tile_attend_productkeys_pl_kernel(
                 nc.tensor.transpose(turned[:, t, :], shares[:, t, :], ident[:])
             w_turned.append(turned)
 
-        v_grouped = tile([P, PACK * I], BF16, "v_grouped", tag="rounded")
+        v_grouped = tile([P, PACK * I], BF16, "v_grouped", tag="pool_rows1")
         for t in range(PACK):
             turn_values(t, v_grouped[:, t * I : (t + 1) * I])
 

@@ -22,6 +22,7 @@ P = 128
 PACK = 4
 BANK = 512
 HALVES = Q // P
+LAST_SHARE = 256
 
 
 def tile_attend_productkeys_pl_kernel(
@@ -46,37 +47,37 @@ def tile_attend_productkeys_pl_kernel(
         book2 = tile([P, V], U32, "book2")
         book_scales = [tile([P, U], U8, f"book_scales{n}") for n in range(2)]
         lists = [keep.tile([P, I // 16], U16, name=f"list{n}") for n in range(3)]
-        pool_rows = [tile([P, T], F32, f"pool_rows{t}") for t in range(PACK - 1)]
-        pool_rows.append(on_last_values([P, T], F32, "pool_rows3", 0))
+        pool_rows = [
+            tile([P, T], F32, "pool_rows0"), on_last_values([P, T], F32, "pool_rows1", 14336),
+            tile([P, T], F32, "pool_rows2"), on_last_values([P, T], F32, "pool_rows3", 0),
+        ]
         size_cols = on_last_values([P, PACK], F32, "size_cols", 4 * T)
         vals_by_place = vals.rearrange("(p t) n -> t p n", t=PACK)
 
-        def load_scales(plane, rows):
+        def load_scales(plane, rows, first):
             for quad in range(4):
                 nc.sync.dma_start(
-                    out=plane[32 * quad : 32 * quad + 4, :].bitcast(I32),
+                    out=plane[32 * quad + first : 32 * quad + first + 4, :].bitcast(I32),
                     in_=rows[0, 4 * quad : 4 * quad + 4, :].bitcast(I32),
                 )
 
         nc.sync.dma_start(out=q_raw[0][:], in_=query.rearrange("(p t) q -> p t q", t=PACK))
         nc.sync.dma_start(out=book1[:].bitcast(I32), in_=sub1_words[0].bitcast(I32))
-        load_scales(book_scales[0], sub1_scales)
+        load_scales(book_scales[0], sub1_scales, 0)
         nc.sync.dma_start(out=q_raw[1][:], in_=query2.rearrange("(p t) q -> p t q", t=PACK))
         nc.sync.dma_start(out=book2[:].bitcast(I32), in_=sub2_words[0].rearrange("p n t -> p (n t)").bitcast(I32))
         nc.sync.dma_start(lists[0][:], offs)
-        load_scales(book_scales[1], sub2_scales)
+        load_scales(book_scales[1], sub2_scales, 4)
         nc.sync.dma_start(out=pool_rows[0][:], in_=vals_by_place[0])
         nc.sync.dma_start(lists[1][:], offs2)
         nc.sync.dma_start(lists[2][:], offs3)
         nc.sync.dma_start(out=pool_rows[1][:], in_=vals_by_place[1])
+        nc.sync.dma_start(out=size_cols[:], in_=size.rearrange("o (p t) -> p (o t)", t=PACK))
         nc.sync.dma_start(out=pool_rows[2][:], in_=vals_by_place[2])
         nc.sync.dma_start(out=pool_rows[3][:], in_=vals_by_place[3])
-        nc.sync.dma_start(out=size_cols[:], in_=size.rearrange("o (p t) -> p (o t)", t=PACK))
 
         ident = tile([P, P], F32, "ident")
         make_identity(nc, ident[:])
-        minus_one = tile([P, 1], F32, "minus_one")
-        nc.gpsimd.memset(minus_one[:], -1.0)
 
         q_codes, q_scales = [], []
         for n in range(2):
@@ -113,31 +114,34 @@ def tile_attend_productkeys_pl_kernel(
                     bank = sums.tile([P, BANK], F32, name="bank")
                     nc.tensor.matmul_mx(
                         out=bank[:], lhsT=q_codes[n][:, rows].bitcast(FP8X4), lhsT_scale=q_scales[n][:, rows],
-                        rhs=keys, rhs_scale=book_scales[n][:, cols], start=True, stop=True,
+                        rhs=keys, rhs_scale=book_scales[n][4 * n :, cols], start=True, stop=True,
                     )
                     nc.scalar.copy(out=whole[:, cols], in_=bank[:])
                 scores[n, h] = whole
 
-        picked = [tile([P, I], BF16, f"picked{t}") for t in range(PACK)]
+        picked = [tile([P, I], BF16, f"picked{t}") for t in range(2)]
+        picked.append(None)
+        picked.append(tile([P, I], BF16, "picked3"))
 
-        def turn_values(t, grouped):
-            words = picked[t][:].bitcast(F32)
+        def turn(source, grouped, copy):
+            words = source.bitcast(F32)
             turned = turns.tile([P, 2, P], F32, name="turned")
             for u in range(2):
                 nc.tensor.transpose(turned[:, u, :], words[:, u : I // 2 : 2], ident[:])
-            nc.scalar.copy(
+            copy(
                 out=grouped.bitcast(F32).rearrange("p (c u) -> p c u", u=2),
                 in_=turned[:].rearrange("p u c -> p c u"),
             )
 
-        def quantise(grouped, name, codes):
-            width = grouped.shape[1] // PACK
-            scales = tile([P, width], U8, name + "_scales")
-            nc.vector.quantize_mx(out=codes[:, :].bitcast(FP8X4), scales=scales[:], in_=grouped)
-            return [(codes[:, c : c + P].bitcast(FP8X4), scales[:, c : c + P]) for c in range(0, width, P)]
+        def quantise(grouped, codes, scales):
+            nc.vector.quantize_mx(out=codes.bitcast(FP8X4), scales=scales, in_=grouped)
 
         for t in (0, 1):
             nc.scalar.activation(out=picked[t][:], in_=pool_rows[t][:].indirect(lists[2][:]), func=ACT.Copy)
+
+        size_spread = sums.tile([P, PACK, P], F32, name="bank")
+        for t in range(PACK):
+            nc.tensor.transpose(size_spread[:, t, :], size_cols[:, t : t + 1].to_broadcast([P, P]), ident[:])
 
         first = []
         for h in range(HALVES):
@@ -145,93 +149,102 @@ def tile_attend_productkeys_pl_kernel(
             nc.vector.tensor_copy(out=picked_b[:], in_=scores[0, h][:].indirect(lists[0][:]))
             first.append(picked_b)
 
-        logits = tile([P, HALVES, I], F32, "logits")
+        logits = [on_last_values([P, I], F32, "logits0", 9216), tile([P, I], F32, "logits1")]
         for h in range(HALVES):
             nc.vector.tensor_tensor(
-                out=logits[:, h, :], in0=scores[1, h][:].indirect(lists[1][:]), in1=first[h][:], op=ALU.add
+                out=logits[h][:], in0=scores[1, h][:].indirect(lists[1][:]), in1=first[h][:], op=ALU.add
             )
         neg_max = tile([P, HALVES], F32, "neg_max")
         for h in range(HALVES):
             nc.vector.tensor_reduce(
-                out=neg_max[:, h : h + 1], in_=logits[:, h, :], axis=AXIS.X, op=ALU.max, negate=True
+                out=neg_max[:, h : h + 1], in_=logits[h][:], axis=AXIS.X, op=ALU.max, negate=True
             )
 
-        expd = tile([P, HALVES, I], F32, "expd", tag="pool_rows1")
-        total = tile([P, HALVES], F32, "total")
+        expd = on_last_values([P, HALVES, I], F32, "expd", 14336)
+        totals = [tile([P, 1], F32, f"total{h}") for h in range(HALVES)]
         for h in range(HALVES):
             nc.scalar.activation(
-                out=expd[:, h, :], in_=logits[:, h, :], func=ACT.Exp, bias=neg_max[:, h : h + 1], scale=1.0,
-                accum_out=total[:, h : h + 1],
+                out=expd[:, h, :], in_=logits[h][:], func=ACT.Exp, bias=neg_max[:, h : h + 1], scale=1.0,
+                accum_out=totals[h][:],
             )
-        nc.vector.tensor_copy(out=picked[2][:], in_=pool_rows[2][:].indirect(lists[2][:]))
-        inv = tile([P, HALVES], F32, "inv")
-        for h in range(HALVES):
-            nc.gpsimd.tensor_tensor(out=inv[:, h : h + 1], in0=total[:, h : h + 1], in1=minus_one[:], op=ALU.pow)
-        nc.vector.tensor_copy(out=picked[3][:], in_=pool_rows[3][:].indirect(lists[2][:]))
+        picked[2] = on_last_values([P, I], BF16, "picked2", 10240)
+        nc.scalar.activation(out=picked[2][:], in_=pool_rows[2][:].indirect(lists[2][:]), func=ACT.Copy)
 
-        w_turned = []
+        v_codes = [tile([P, P], U32, f"v_codes{t}") for t in range(PACK)]
+        v_scales = [tile([P, P], U8, f"v_scales{t}") for t in range(PACK)]
+        v_first = tile([P, I], BF16, "v_first", tag="picked_b1")
+        turn(picked[0][:], v_first[:], nc.vector.tensor_copy)
+        quantise(v_first[:], v_codes[0][:], v_scales[0][:])
+        v_second = on_last_values([P, I], BF16, "v_second", 9216)
+
+        invs = [tile([P, 1], F32, f"inv{h}") for h in range(HALVES)]
+        weights = [tile([P, I], BF16, f"weights{h}") for h in range(HALVES)]
         for h in range(HALVES):
-            shares = tile([P, PACK, P], F32, f"shares{h}")
-            nc.scalar.activation(
-                out=shares[:].rearrange("p t (c i) -> p c t i", i=4),
-                in_=expd[:, h, :].rearrange("p (c i t) -> p c t i", i=4, t=PACK),
-                func=ACT.Copy, scale=inv[:, h : h + 1],
+            nc.vector.reciprocal(out=invs[h][:], in_=totals[h][:])
+            if h == 0:
+                turn(picked[1][:], v_second[:], nc.vector.tensor_copy)
+            else:
+                quantise(v_second[:], v_codes[1][:], v_scales[1][:])
+            nc.vector.scalar_tensor_tensor(
+                out=weights[h][:].rearrange("q (p t) -> q p t", t=PACK),
+                in0=expd[:, h, :].rearrange("q (p t) -> q p t", t=PACK), scalar=invs[h][:],
+                in1=size_spread[:].rearrange("q t p -> q p t"), op0=ALU.mult, op1=ALU.mult,
             )
-            turned = sums.tile([P, PACK, P], F32, name="bank")
-            for t in range(PACK):
-                nc.tensor.transpose(turned[:, t, :], shares[:, t, :], ident[:])
-            w_turned.append(turned)
 
-        v_grouped = tile([P, PACK * I], BF16, "v_grouped", tag="pool_rows1")
-        for t in range(PACK):
-            turn_values(t, v_grouped[:, t * I : (t + 1) * I])
+        w_grouped = [tile([P, I], BF16, "w_grouped0", tag="total1"), on_last_values([P, I], BF16, "w_grouped1", 0)]
+        w_codes = on_last_values([P, Q], U32, "w_codes", 2048)
+        w_scales = tile([P, Q], U8, "w_scales")
+        turn(weights[0][:], w_grouped[0][:], nc.vector.tensor_copy)
+        nc.vector.tensor_copy(
+            out=picked[3][:, :LAST_SHARE], in_=pool_rows[3][:].indirect(lists[2][:, : LAST_SHARE // 16])
+        )
+        nc.scalar.activation(
+            out=picked[3][:, LAST_SHARE:], in_=pool_rows[3][:].indirect(lists[2][:, LAST_SHARE // 16 :]), func=ACT.Copy
+        )
+        turn(weights[1][:], w_grouped[1][:], nc.scalar.copy)
+        quantise(w_grouped[0][:], w_codes[:, :P], w_scales[:, :P])
+        v_third = on_last_values([P, I], BF16, "v_third", 1024)
+        turn(picked[2][:], v_third[:], nc.vector.tensor_copy)
+        v_last = tile([P, I], BF16, "v_last")
+        turn(picked[3][:], v_last[:], nc.scalar.copy)
+        quantise(w_grouped[1][:], w_codes[:, P:], w_scales[:, P:])
+        quantise(v_third[:], v_codes[2][:], v_scales[2][:])
+        quantise(v_last[:], v_codes[3][:], v_scales[3][:])
+        v_mx = [(v_codes[t][:], v_scales[t][:]) for t in range(PACK)]
 
-        w_grouped = tile([P, HALVES, P, PACK], BF16, "w_grouped")
-        for h in range(HALVES):
-            nc.vector.tensor_tensor(
-                out=w_grouped[:, h, :, :], in0=w_turned[h][:].rearrange("p t q -> p q t"),
-                in1=size_cols[:].unsqueeze(1).to_broadcast([P, P, PACK]), op=ALU.mult,
+        def multiply(out, t, cols):
+            nc.tensor.matmul_mx(
+                out=out, lhsT=v_mx[t][0].bitcast(FP8X4), lhsT_scale=v_mx[t][1],
+                rhs=w_codes[:, cols].bitcast(FP8X4), rhs_scale=w_scales[:, cols], start=True, stop=True,
             )
-        w_mx = quantise(w_grouped[:, 0, :, :].rearrange("p q t -> p (q t)"), "w0", tile([P, P], U32, "w0_codes"))
-        v_codes = on_last_values([P, PACK * P], U32, "v_codes", 4 * T)
-        v_mx = quantise(v_grouped[:, : 2 * I], "v_first", v_codes[:, : 2 * P])
-        v_mx = v_mx + quantise(v_grouped[:, 2 * I :], "v_second", v_codes[:, 2 * P :])
-        w_mx = w_mx + quantise(w_grouped[:, 1, :, :].rearrange("p q t -> p (q t)"), "w1", tile([P, P], U32, "w1_codes"))
 
         o_codes = tile([P, Q], U32, "o_codes")
         o_scales = tile([P, Q], U8, "o_scales")
         out_rows = out_0.rearrange("(p t) q -> p t q", t=PACK)
         out_words = out_1[0].rearrange("p c t -> p (c t)").bitcast(I32)
         o_grouped = tile([P, Q, PACK], BF16, "o_grouped")
-        for h in range(HALVES):
-            cols = slice(h * P, (h + 1) * P)
-            o_sb = tile([P, PACK, P], F32, f"o_sb{h}")
-            if h == 1:
-                whole_bank = turns.tile([P, PACK, P], F32, name="turned")
-                for t in range(PACK):
-                    nc.tensor.matmul_mx(
-                        out=whole_bank[:, t, :], lhsT=v_mx[t][0], lhsT_scale=v_mx[t][1],
-                        rhs=w_mx[h][0], rhs_scale=w_mx[h][1], start=True, stop=True,
-                    )
-                nc.vector.tensor_copy(out=o_grouped[:, cols, :], in_=whole_bank[:].rearrange("p t q -> p q t"))
-            for u in range(2):
-                bank = sums.tile([P, 2, P], F32, name="bank")
-                for e in range(2):
-                    nc.tensor.matmul_mx(
-                        out=bank[:, e, :], lhsT=v_mx[2 * u + e][0], lhsT_scale=v_mx[2 * u + e][1],
-                        rhs=w_mx[h][0], rhs_scale=w_mx[h][1], start=True, stop=True,
-                    )
-                places = slice(2 * u, 2 * u + 2)
-                nc.scalar.copy(out=o_sb[:, places, :], in_=bank[:])
-                if h == 1:
-                    nc.sync.dma_start(out=out_rows[:, places, cols], in_=o_sb[:, places, :])
-            if h == 0:
-                nc.sync.dma_start(out=out_rows[:, :, cols], in_=o_sb[:])
-            if h == 0:
-                nc.vector.tensor_copy(
-                    out=o_grouped[:, cols, :].rearrange("p (c i) t -> p c t i", i=4),
-                    in_=o_sb[:].rearrange("p t (c i) -> p c t i", i=4),
-                )
+        o_sb = tile([P, PACK, Q], F32, "o_sb")
+        halves = [slice(h * P, (h + 1) * P) for h in range(HALVES)]
+        for cols in halves:
+            bank = sums.tile([P, 2, P], F32, name="bank")
+            for t in range(2):
+                multiply(bank[:, t, :], t, cols)
+            nc.scalar.copy(out=o_sb[:, :2, cols], in_=bank[:])
+        nc.sync.dma_start(out=out_rows[:, :2, :], in_=o_sb[:, :2, :])
+        bank = sums.tile([P, Q], F32, name="bank")
+        multiply(bank[:], 2, slice(0, Q))
+        nc.vector.tensor_copy(out=o_sb[:, 2, :], in_=bank[:])
+        nc.sync.dma_start(out=out_rows[:, 2, :], in_=o_sb[:, 2, :])
+        for cols in halves:
+            bank = turns.tile([P, P], F32, name="turned")
+            multiply(bank[:], 3, cols)
+            nc.scalar.copy(out=o_sb[:, 3, cols], in_=bank[:])
+        nc.sync.dma_start(out=out_rows[:, 3, :], in_=o_sb[:, 3, :])
+        for cols in halves:
+            nc.vector.tensor_copy(
+                out=o_grouped[:, cols, :].rearrange("p (c i) t -> p c t i", i=4),
+                in_=o_sb[:, :, cols].rearrange("p t (c i) -> p c t i", i=4),
+            )
         for h in range(HALVES):
             cols = slice(h * P, (h + 1) * P)
             nc.vector.quantize_mx(

@@ -123,11 +123,12 @@ def tile_attend_productkeys_pl_kernel(
         picked.append(None)
         picked.append(tile([P, I], BF16, "picked3"))
 
-        def turn(source, grouped, copy):
+        def turn(source, grouped, copy, dealt=False):
             words = source.bitcast(F32)
             turned = turns.tile([P, 2, P], F32, name="turned")
             for u in range(2):
-                nc.tensor.transpose(turned[:, u, :], words[:, u : I // 2 : 2], ident[:])
+                taken = words[:, u * P : (u + 1) * P] if dealt else words[:, u : I // 2 : 2]
+                nc.tensor.transpose(turned[:, u, :], taken, ident[:])
             copy(
                 out=grouped.bitcast(F32).rearrange("p (c u) -> p c u", u=2),
                 in_=turned[:].rearrange("p u c -> p c u"),
@@ -139,9 +140,10 @@ def tile_attend_productkeys_pl_kernel(
         for t in (0, 1):
             nc.scalar.activation(out=picked[t][:], in_=pool_rows[t][:].indirect(lists[2][:]), func=ACT.Copy)
 
-        size_spread = sums.tile([P, PACK, P], F32, name="bank")
+        size_spread = sums.tile([P, 2, 2 * P], F32, name="bank")
         for t in range(PACK):
-            nc.tensor.transpose(size_spread[:, t, :], size_cols[:, t : t + 1].to_broadcast([P, P]), ident[:])
+            place = size_spread[:].rearrange("q u (p e) -> q u p e", e=2)[:, t // 2, :, t % 2]
+            nc.tensor.transpose(place, size_cols[:, t : t + 1].to_broadcast([P, P]), ident[:])
 
         first = []
         for h in range(HALVES):
@@ -164,7 +166,8 @@ def tile_attend_productkeys_pl_kernel(
         totals = [tile([P, 1], F32, f"total{h}") for h in range(HALVES)]
         for h in range(HALVES):
             nc.scalar.activation(
-                out=expd[:, h, :], in_=logits[h][:], func=ACT.Exp, bias=neg_max[:, h : h + 1], scale=1.0,
+                out=expd[:, h, :].rearrange("q (u p e) -> q p u e", u=2, e=2),
+                in_=logits[h][:].rearrange("q (p u e) -> q p u e", u=2, e=2), func=ACT.Exp, bias=neg_max[:, h : h + 1], scale=1.0,
                 accum_out=totals[h][:],
             )
         picked[2] = on_last_values([P, I], BF16, "picked2", 10240)
@@ -186,22 +189,21 @@ def tile_attend_productkeys_pl_kernel(
             else:
                 quantise(v_second[:], v_codes[1][:], v_scales[1][:])
             nc.vector.scalar_tensor_tensor(
-                out=weights[h][:].rearrange("q (p t) -> q p t", t=PACK),
-                in0=expd[:, h, :].rearrange("q (p t) -> q p t", t=PACK), scalar=invs[h][:],
-                in1=size_spread[:].rearrange("q t p -> q p t"), op0=ALU.mult, op1=ALU.mult,
+                out=weights[h][:], in0=expd[:, h, :], scalar=invs[h][:],
+                in1=size_spread[:].rearrange("q u c -> q (u c)"), op0=ALU.mult, op1=ALU.mult,
             )
 
         w_grouped = [tile([P, I], BF16, "w_grouped0", tag="total1"), on_last_values([P, I], BF16, "w_grouped1", 0)]
         w_codes = on_last_values([P, Q], U32, "w_codes", 2048)
         w_scales = tile([P, Q], U8, "w_scales")
-        turn(weights[0][:], w_grouped[0][:], nc.vector.tensor_copy)
+        turn(weights[0][:], w_grouped[0][:], nc.vector.tensor_copy, dealt=True)
         nc.vector.tensor_copy(
             out=picked[3][:, :LAST_SHARE], in_=pool_rows[3][:].indirect(lists[2][:, : LAST_SHARE // 16])
         )
         nc.scalar.activation(
             out=picked[3][:, LAST_SHARE:], in_=pool_rows[3][:].indirect(lists[2][:, LAST_SHARE // 16 :]), func=ACT.Copy
         )
-        turn(weights[1][:], w_grouped[1][:], nc.scalar.copy)
+        turn(weights[1][:], w_grouped[1][:], nc.scalar.copy, dealt=True)
         quantise(w_grouped[0][:], w_codes[:, :P], w_scales[:, :P])
         v_third = on_last_values([P, I], BF16, "v_third", 1024)
         turn(picked[2][:], v_third[:], nc.vector.tensor_copy)

@@ -54,20 +54,20 @@ def tile_attend_productkeys_pl_kernel(
         size_cols = on_last_values([P, PACK], F32, "size_cols", 4 * T)
         vals_by_place = vals.rearrange("(p t) n -> t p n", t=PACK)
 
-        def load_scales(plane, rows, first):
-            for quad in range(4):
-                nc.sync.dma_start(
+        def load_scales(plane, rows, first, queues):
+            for quad, queue in enumerate(queues):
+                queue.dma_start(
                     out=plane[32 * quad + first : 32 * quad + first + 4, :].bitcast(I32),
                     in_=rows[0, 4 * quad : 4 * quad + 4, :].bitcast(I32),
                 )
 
         nc.sync.dma_start(out=q_raw[0][:], in_=query.rearrange("(p t) q -> p t q", t=PACK))
         nc.sync.dma_start(out=book1[:].bitcast(I32), in_=sub1_words[0].bitcast(I32))
-        load_scales(book_scales[0], sub1_scales, 0)
+        load_scales(book_scales[0], sub1_scales, 0, (nc.scalar, nc.sync, nc.sync, nc.sync))
         nc.sync.dma_start(out=q_raw[1][:], in_=query2.rearrange("(p t) q -> p t q", t=PACK))
         nc.sync.dma_start(out=book2[:].bitcast(I32), in_=sub2_words[0].rearrange("p n t -> p (n t)").bitcast(I32))
         nc.sync.dma_start(lists[0][:], offs)
-        load_scales(book_scales[1], sub2_scales, 4)
+        load_scales(book_scales[1], sub2_scales, 4, (nc.sync, nc.sync, nc.sync, nc.sync))
         nc.sync.dma_start(out=pool_rows[0][:], in_=vals_by_place[0])
         nc.sync.dma_start(lists[1][:], offs2)
         nc.sync.dma_start(lists[2][:], offs3)

@@ -55,10 +55,9 @@ def tile_attend_productkeys_pl_kernel(
         vals_by_place = vals.rearrange("(p t) n -> t p n", t=PACK)
 
         def load_scales(plane, rows, first, queues):
-            for quad, queue in enumerate(queues):
+            for row, queue in enumerate(queues):
                 queue.dma_start(
-                    out=plane[32 * quad + first : 32 * quad + first + 4, :].bitcast(I32),
-                    in_=rows[0, 4 * quad : 4 * quad + 4, :].bitcast(I32),
+                    out=plane[first + row : P : 32, :].bitcast(I32), in_=rows[0, row : 16 : 4, :].bitcast(I32)
                 )
 
         nc.sync.dma_start(out=q_raw[0][:], in_=query.rearrange("(p t) q -> p t q", t=PACK))

@@ -20,9 +20,10 @@ AXIS = mybir.AxisListType
 
 P = 128
 PACK = 4
-BANK = 512
+PASS = 256
 HALVES = Q // P
 LAST_SHARE = 256
+GROUP_SHARE = 64
 
 
 def tile_attend_productkeys_pl_kernel(
@@ -42,13 +43,13 @@ def tile_attend_productkeys_pl_kernel(
         def on_last_values(shape, dtype, name, offset):
             return shared.tile(shape, dtype, name=name, offset=offset, align_bytes=64)
 
-        q_raw = [tile([P, PACK, Q], F32, f"q_raw{n}") for n in range(2)]
+        q_raw = [tile([P, PACK, Q], F32, "q_raw0"), on_last_values([P, PACK, Q], F32, "q_raw1", 30720)]
         book1 = tile([P, 2 * U], U8, "book1")
         book2 = tile([P, V], U32, "book2")
         book_scales = [tile([P, U], U8, f"book_scales{n}") for n in range(2)]
         lists = [keep.tile([P, I // 16], U16, name=f"list{n}") for n in range(3)]
         pool_rows = [
-            tile([P, T], F32, "pool_rows0"), on_last_values([P, T], F32, "pool_rows1", 14336),
+            on_last_values([P, T], F32, "pool_rows0", 22528), on_last_values([P, T], F32, "pool_rows1", 14336),
             tile([P, T], F32, "pool_rows2"), on_last_values([P, T], F32, "pool_rows3", 0),
         ]
         size_cols = on_last_values([P, PACK], F32, "size_cols", 4 * T)
@@ -63,12 +64,12 @@ def tile_attend_productkeys_pl_kernel(
         nc.sync.dma_start(out=q_raw[0][:], in_=query.rearrange("(p t) q -> p t q", t=PACK))
         nc.sync.dma_start(out=book1[:].bitcast(I32), in_=sub1_words[0].bitcast(I32))
         load_scales(book_scales[0], sub1_scales, 0, (nc.scalar, nc.sync, nc.sync, nc.sync))
+        nc.sync.dma_start(lists[0][:], offs)
         nc.sync.dma_start(out=q_raw[1][:], in_=query2.rearrange("(p t) q -> p t q", t=PACK))
         nc.sync.dma_start(out=book2[:].bitcast(I32), in_=sub2_words[0].rearrange("p n t -> p (n t)").bitcast(I32))
-        nc.sync.dma_start(lists[0][:], offs)
         load_scales(book_scales[1], sub2_scales, 4, (nc.sync, nc.sync, nc.sync, nc.sync))
-        nc.sync.dma_start(out=pool_rows[0][:], in_=vals_by_place[0])
         nc.sync.dma_start(lists[1][:], offs2)
+        nc.sync.dma_start(out=pool_rows[0][:], in_=vals_by_place[0])
         nc.sync.dma_start(lists[2][:], offs3)
         nc.sync.dma_start(out=pool_rows[1][:], in_=vals_by_place[1])
         nc.sync.dma_start(out=size_cols[:], in_=size.rearrange("o (p t) -> p (o t)", t=PACK))
@@ -104,13 +105,13 @@ def tile_attend_productkeys_pl_kernel(
             for h in range(HALVES):
                 rows = slice(h * P, (h + 1) * P)
                 whole = tile([P, U], F32, f"scores{n}_{h}")
-                for c in range(U // BANK):
-                    cols = slice(c * BANK, (c + 1) * BANK)
+                for c in range(U // PASS):
+                    cols = slice(c * PASS, (c + 1) * PASS)
                     if n == 0:
-                        keys = book1[:, 2 * c * BANK : 2 * (c + 1) * BANK].bitcast(FP4X4)
+                        keys = book1[:, 2 * c * PASS : 2 * (c + 1) * PASS].bitcast(FP4X4)
                     else:
                         keys = book2[:, cols].bitcast(FP8X4)
-                    bank = sums.tile([P, BANK], F32, name="bank")
+                    bank = sums.tile([P, PASS], F32, name="bank")
                     nc.tensor.matmul_mx(
                         out=bank[:], lhsT=q_codes[n][:, rows].bitcast(FP8X4), lhsT_scale=q_scales[n][:, rows],
                         rhs=keys, rhs_scale=book_scales[n][4 * n :, cols], start=True, stop=True,
@@ -146,7 +147,7 @@ def tile_attend_productkeys_pl_kernel(
 
         first = []
         for h in range(HALVES):
-            picked_b = tile([P, I], F32, f"picked_b{h}", tag="q_raw1" if h == 0 else None)
+            picked_b = on_last_values([P, I], F32, f"picked_b{h}", 30720 + 4 * I * h)
             nc.vector.tensor_copy(out=picked_b[:], in_=scores[0, h][:].indirect(lists[0][:]))
             first.append(picked_b)
 
@@ -155,7 +156,7 @@ def tile_attend_productkeys_pl_kernel(
             nc.vector.tensor_tensor(
                 out=logits[h][:], in0=scores[1, h][:].indirect(lists[1][:]), in1=first[h][:], op=ALU.add
             )
-        neg_max = tile([P, HALVES], F32, "neg_max")
+        neg_max = on_last_values([P, HALVES], F32, "neg_max", 22528)
         for h in range(HALVES):
             nc.vector.tensor_reduce(
                 out=neg_max[:, h : h + 1], in_=logits[h][:], axis=AXIS.X, op=ALU.max, negate=True
@@ -174,7 +175,7 @@ def tile_attend_productkeys_pl_kernel(
 
         v_codes = [tile([P, P], U32, f"v_codes{t}") for t in range(PACK)]
         v_scales = [tile([P, P], U8, f"v_scales{t}") for t in range(PACK)]
-        v_first = tile([P, I], BF16, "v_first", tag="picked_b1")
+        v_first = on_last_values([P, I], BF16, "v_first", 30720 + 4 * I)
         turn(picked[0][:], v_first[:], nc.vector.tensor_copy)
         quantise(v_first[:], v_codes[0][:], v_scales[0][:])
         v_second = on_last_values([P, I], BF16, "v_second", 9216)
@@ -241,8 +242,11 @@ def tile_attend_productkeys_pl_kernel(
             multiply(bank[:], 3, cols)
             nc.scalar.copy(out=o_sb[:, 3, cols], in_=bank[:])
         nc.sync.dma_start(out=out_rows[:, 3, :], in_=o_sb[:, 3, :])
-        for cols in halves:
-            nc.vector.tensor_copy(
+        for copy, cols in (
+            (nc.vector.tensor_copy, slice(0, P - GROUP_SHARE)), (nc.scalar.copy, slice(P - GROUP_SHARE, P)),
+            (nc.vector.tensor_copy, halves[1]),
+        ):
+            copy(
                 out=o_grouped[:, cols, :].rearrange("p (c i) t -> p c t i", i=4),
                 in_=o_sb[:, :, cols].rearrange("p t (c i) -> p c t i", i=4),
             )

@@ -203,10 +203,10 @@ def tile_attend_productkeys_pl_kernel(
         nc.scalar.activation(
             out=picked[3][:, LAST_SHARE:], in_=pool_rows[3][:].indirect(lists[2][:, LAST_SHARE // 16 :]), func=ACT.Copy
         )
-        turn(weights[1][:], w_grouped[1][:], nc.scalar.copy, dealt=True)
+        turn(weights[1][:], w_grouped[1][:], nc.vector.tensor_copy, dealt=True)
         quantise(w_grouped[0][:], w_codes[:, :P], w_scales[:, :P])
         v_third = on_last_values([P, I], BF16, "v_third", 1024)
-        turn(picked[2][:], v_third[:], nc.vector.tensor_copy)
+        turn(picked[2][:], v_third[:], nc.scalar.copy)
         v_last = tile([P, I], BF16, "v_last")
         turn(picked[3][:], v_last[:], nc.scalar.copy)
         quantise(w_grouped[1][:], w_codes[:, P:], w_scales[:, P:])

@@ -46,7 +46,7 @@ def tile_attend_productkeys_pl_kernel(
         q_raw = [tile([P, PACK, Q], F32, "q_raw0"), on_last_values([P, PACK, Q], F32, "q_raw1", 30720)]
         book1 = tile([P, 2 * U], U8, "book1")
         book2 = tile([P, V], U32, "book2")
-        book_scales = [tile([P, U], U8, f"book_scales{n}") for n in range(2)]
+        book_scales = [tile([P, U], U8, "book_scales0"), tile([P, PASS], U8, "book_scales1")]
         lists = [keep.tile([P, I // 16], U16, name=f"list{n}") for n in range(3)]
         pool_rows = [
             on_last_values([P, T], F32, "pool_rows0", 22528), on_last_values([P, T], F32, "pool_rows1", 14336),
@@ -67,7 +67,11 @@ def tile_attend_productkeys_pl_kernel(
         nc.sync.dma_start(lists[0][:], offs)
         nc.sync.dma_start(out=q_raw[1][:], in_=query2.rearrange("(p t) q -> p t q", t=PACK))
         nc.sync.dma_start(out=book2[:].bitcast(I32), in_=sub2_words[0].rearrange("p n t -> p (n t)").bitcast(I32))
-        load_scales(book_scales[1], sub2_scales, 4, (nc.sync, nc.sync, nc.sync, nc.sync))
+        for quad in range(4):
+            nc.sync.dma_start(
+                out=book_scales[1][32 * quad : 32 * quad + 16, :].bitcast(I32),
+                in_=sub2_scales[0, 4 * quad : 4 * quad + 4, :].bitcast(I32).rearrange("r (a c) -> a r c", a=4),
+            )
         nc.sync.dma_start(lists[1][:], offs2)
         nc.sync.dma_start(out=pool_rows[0][:], in_=vals_by_place[0])
         nc.sync.dma_start(lists[2][:], offs3)
@@ -109,12 +113,14 @@ def tile_attend_productkeys_pl_kernel(
                     cols = slice(c * PASS, (c + 1) * PASS)
                     if n == 0:
                         keys = book1[:, 2 * c * PASS : 2 * (c + 1) * PASS].bitcast(FP4X4)
+                        key_scales = book_scales[0][:, cols]
                     else:
                         keys = book2[:, cols].bitcast(FP8X4)
+                        key_scales = book_scales[1][4 * c :, :]
                     bank = sums.tile([P, PASS], F32, name="bank")
                     nc.tensor.matmul_mx(
                         out=bank[:], lhsT=q_codes[n][:, rows].bitcast(FP8X4), lhsT_scale=q_scales[n][:, rows],
-                        rhs=keys, rhs_scale=book_scales[n][4 * n :, cols], start=True, stop=True,
+                        rhs=keys, rhs_scale=key_scales, start=True, stop=True,
                     )
                     nc.scalar.copy(out=whole[:, cols], in_=bank[:])
                 scores[n, h] = whole

from contextlib import ExitStack

import concourse.mybir as mybir
from concourse.masks import make_identity

D, K, U, V, T, I, Q, E = 512, 512, 1024, 1024, 2048, 512, 256, 512
FLOPS = 2 * D * Q * U + 2 * K * Q * V + 2 * I * E * Q

F32 = mybir.dt.float32
BF16 = mybir.dt.bfloat16
I32 = mybir.dt.int32
U32 = mybir.dt.uint32
U16 = mybir.dt.uint16
U8 = mybir.dt.uint8
FP8X4 = mybir.dt.float8_e4m3fn_x4
FP4X4 = mybir.dt.float4_e2m1fn_x4
ALU = mybir.AluOpType
ACT = mybir.ActivationFunctionType
AXIS = mybir.AxisListType

P = 128
PACK = 4
PASS = 256
HALVES = Q // P
LAST_SHARE = 256
GROUP_SHARE = 64


def tile_attend_productkeys_pl_kernel(
    tc, query, query2, sub1_words, sub1_scales, sub2_words, sub2_scales, size, vals, offs, offs2, offs3,
    out_0, out_1, out_2,
):
    nc = tc.nc
    with ExitStack() as ctx:
        keep = ctx.enter_context(tc.tile_pool(name="keep", bufs=1))
        shared = ctx.enter_context(tc.tile_pool(name="shared", bufs=1))
        sums = ctx.enter_context(tc.psum_pool(name="sums", bufs=4))
        turns = ctx.enter_context(tc.psum_pool(name="turns", bufs=4))

        def tile(shape, dtype, name, tag=None):
            return keep.tile(shape, dtype, name=name, tag=tag or name, align_bytes=64)

        def on_last_values(shape, dtype, name, offset):
            return shared.tile(shape, dtype, name=name, offset=offset, align_bytes=64)

        q_raw = [tile([P, PACK, Q], F32, "q_raw0"), on_last_values([P, PACK, Q], F32, "q_raw1", 30720)]
        book1 = tile([P, 2 * U], U8, "book1")
        book2 = tile([P, V], U32, "book2")
        book_scales = [tile([P, U], U8, "book_scales0"), tile([P, PASS], U8, "book_scales1")]
        lists = [keep.tile([P, I // 16], U16, name=f"list{n}") for n in range(3)]
        pool_rows = [
            on_last_values([P, T], F32, "pool_rows0", 22528), on_last_values([P, T], F32, "pool_rows1", 14336),
            tile([P, T], F32, "pool_rows2"), on_last_values([P, T], F32, "pool_rows3", 0),
        ]
        size_cols = on_last_values([P, PACK], F32, "size_cols", 4 * T)
        vals_by_place = vals.rearrange("(p t) n -> t p n", t=PACK)

        def load_scales(plane, rows, first, queues):
            for row, queue in enumerate(queues):
                queue.dma_start(
                    out=plane[first + row : P : 32, :].bitcast(I32), in_=rows[0, row : 16 : 4, :].bitcast(I32)
                )

        nc.sync.dma_start(out=q_raw[0][:], in_=query.rearrange("(p t) q -> p t q", t=PACK))
        nc.sync.dma_start(out=book1[:].bitcast(I32), in_=sub1_words[0].bitcast(I32))
        load_scales(book_scales[0], sub1_scales, 0, (nc.scalar, nc.sync, nc.sync, nc.sync))
        nc.sync.dma_start(lists[0][:], offs)
        nc.sync.dma_start(out=q_raw[1][:], in_=query2.rearrange("(p t) q -> p t q", t=PACK))
        nc.sync.dma_start(out=book2[:].bitcast(I32), in_=sub2_words[0].rearrange("p n t -> p (n t)").bitcast(I32))
        for quad in range(4):
            nc.sync.dma_start(
                out=book_scales[1][32 * quad : 32 * quad + 16, :].bitcast(I32),
                in_=sub2_scales[0, 4 * quad : 4 * quad + 4, :].bitcast(I32).rearrange("r (a c) -> a r c", a=4),
            )
        nc.sync.dma_start(lists[1][:], offs2)
        nc.sync.dma_start(out=pool_rows[0][:], in_=vals_by_place[0])
        nc.sync.dma_start(lists[2][:], offs3)
        nc.sync.dma_start(out=pool_rows[1][:], in_=vals_by_place[1])
        nc.sync.dma_start(out=size_cols[:], in_=size.rearrange("o (p t) -> p (o t)", t=PACK))
        nc.sync.dma_start(out=pool_rows[2][:], in_=vals_by_place[2])
        nc.sync.dma_start(out=pool_rows[3][:], in_=vals_by_place[3])

        ident = tile([P, P], F32, "ident")
        make_identity(nc, ident[:])

        q_codes, q_scales = [], []
        for n in range(2):
            grouped = tile([P, Q, PACK], BF16, f"q_grouped{n}")
            codes = tile([P, Q], U32, f"q_codes{n}")
            scales = tile([P, Q], U8, f"q_scales{n}")
            for h in range(HALVES):
                rows = slice(h * P, (h + 1) * P)
                cast = nc.scalar.copy if (n, h) == (0, 1) else nc.vector.tensor_copy
                cast(
                    out=grouped[:, rows, :].rearrange("p (c i) t -> p c t i", i=4),
                    in_=q_raw[n][:, :, rows].rearrange("p t (c i) -> p c t i", i=4),
                )
            for h in range(HALVES):
                rows = slice(h * P, (h + 1) * P)
                nc.vector.quantize_mx(
                    out=codes[:, rows].bitcast(FP8X4), scales=scales[:, rows],
                    in_=grouped[:, rows, :].rearrange("p q t -> p (q t)"),
                )
            q_codes.append(codes)
            q_scales.append(scales)

        scores = {}
        for n in range(2):
            for h in range(HALVES):
                rows = slice(h * P, (h + 1) * P)
                whole = tile([P, U], F32, f"scores{n}_{h}")
                for c in range(U // PASS):
                    cols = slice(c * PASS, (c + 1) * PASS)
                    if n == 0:
                        keys = book1[:, 2 * c * PASS : 2 * (c + 1) * PASS].bitcast(FP4X4)
                        key_scales = book_scales[0][:, cols]
                    else:
                        keys = book2[:, cols].bitcast(FP8X4)
                        key_scales = book_scales[1][4 * c :, :]
                    bank = sums.tile([P, PASS], F32, name="bank")
                    nc.tensor.matmul_mx(
                        out=bank[:], lhsT=q_codes[n][:, rows].bitcast(FP8X4), lhsT_scale=q_scales[n][:, rows],
                        rhs=keys, rhs_scale=key_scales, start=True, stop=True,
                    )
                    nc.scalar.copy(out=whole[:, cols], in_=bank[:])
                scores[n, h] = whole

        picked = [tile([P, I], BF16, f"picked{t}") for t in range(2)]
        picked.append(None)
        picked.append(tile([P, I], BF16, "picked3"))

        def turn(source, grouped, copy, dealt=False):
            words = source.bitcast(F32)
            turned = turns.tile([P, 2, P], F32, name="turned")
            for u in range(2):
                taken = words[:, u * P : (u + 1) * P] if dealt else words[:, u : I // 2 : 2]
                nc.tensor.transpose(turned[:, u, :], taken, ident[:])
            copy(
                out=grouped.bitcast(F32).rearrange("p (c u) -> p c u", u=2),
                in_=turned[:].rearrange("p u c -> p c u"),
            )

        def quantise(grouped, codes, scales):
            nc.vector.quantize_mx(out=codes.bitcast(FP8X4), scales=scales, in_=grouped)

        for t in (0, 1):
            nc.scalar.activation(out=picked[t][:], in_=pool_rows[t][:].indirect(lists[2][:]), func=ACT.Copy)

        size_spread = sums.tile([P, 2, 2 * P], F32, name="bank")
        for t in range(PACK):
            place = size_spread[:].rearrange("q u (p e) -> q u p e", e=2)[:, t // 2, :, t % 2]
            nc.tensor.transpose(place, size_cols[:, t : t + 1].to_broadcast([P, P]), ident[:])

        first = []
        for h in range(HALVES):
            picked_b = on_last_values([P, I], F32, f"picked_b{h}", 30720 + 4 * I * h)
            nc.vector.tensor_copy(out=picked_b[:], in_=scores[0, h][:].indirect(lists[0][:]))
            first.append(picked_b)

        logits = [on_last_values([P, I], F32, "logits0", 9216), tile([P, I], F32, "logits1")]
        for h in range(HALVES):
            nc.vector.tensor_tensor(
                out=logits[h][:], in0=scores[1, h][:].indirect(lists[1][:]), in1=first[h][:], op=ALU.add
            )
        neg_max = on_last_values([P, HALVES], F32, "neg_max", 22528)
        for h in range(HALVES):
            nc.vector.tensor_reduce(
                out=neg_max[:, h : h + 1], in_=logits[h][:], axis=AXIS.X, op=ALU.max, negate=True
            )

        expd = on_last_values([P, HALVES, I], F32, "expd", 14336)
        totals = [tile([P, 1], F32, f"total{h}") for h in range(HALVES)]
        for h in range(HALVES):
            nc.scalar.activation(
                out=expd[:, h, :].rearrange("q (u p e) -> q p u e", u=2, e=2),
                in_=logits[h][:].rearrange("q (p u e) -> q p u e", u=2, e=2), func=ACT.Exp, bias=neg_max[:, h : h + 1], scale=1.0,
                accum_out=totals[h][:],
            )
        picked[2] = on_last_values([P, I], BF16, "picked2", 10240)
        nc.scalar.activation(out=picked[2][:], in_=pool_rows[2][:].indirect(lists[2][:]), func=ACT.Copy)

        v_codes = [tile([P, P], U32, f"v_codes{t}") for t in range(PACK)]
        v_scales = [tile([P, P], U8, f"v_scales{t}") for t in range(PACK)]
        v_first = on_last_values([P, I], BF16, "v_first", 30720 + 4 * I)
        turn(picked[0][:], v_first[:], nc.vector.tensor_copy)
        quantise(v_first[:], v_codes[0][:], v_scales[0][:])
        v_second = on_last_values([P, I], BF16, "v_second", 9216)

        invs = [tile([P, 1], F32, f"inv{h}") for h in range(HALVES)]
        weights = [tile([P, I], BF16, f"weights{h}") for h in range(HALVES)]
        for h in range(HALVES):
            nc.vector.reciprocal(out=invs[h][:], in_=totals[h][:])
            if h == 0:
                turn(picked[1][:], v_second[:], nc.vector.tensor_copy)
            else:
                quantise(v_second[:], v_codes[1][:], v_scales[1][:])
            nc.vector.scalar_tensor_tensor(
                out=weights[h][:], in0=expd[:, h, :], scalar=invs[h][:],
                in1=size_spread[:].rearrange("q u c -> q (u c)"), op0=ALU.mult, op1=ALU.mult,
            )

        w_grouped = [tile([P, I], BF16, "w_grouped0", tag="total1"), on_last_values([P, I], BF16, "w_grouped1", 0)]
        w_codes = on_last_values([P, Q], U32, "w_codes", 2048)
        w_scales = tile([P, Q], U8, "w_scales")
        turn(weights[0][:], w_grouped[0][:], nc.vector.tensor_copy, dealt=True)
        nc.vector.tensor_copy(
            out=picked[3][:, :LAST_SHARE], in_=pool_rows[3][:].indirect(lists[2][:, : LAST_SHARE // 16])
        )
        nc.scalar.activation(
            out=picked[3][:, LAST_SHARE:], in_=pool_rows[3][:].indirect(lists[2][:, LAST_SHARE // 16 :]), func=ACT.Copy
        )
        turn(weights[1][:], w_grouped[1][:], nc.vector.tensor_copy, dealt=True)
        quantise(w_grouped[0][:], w_codes[:, :P], w_scales[:, :P])
        v_third = on_last_values([P, I], BF16, "v_third", 1024)
        turn(picked[2][:], v_third[:], nc.scalar.copy)
        v_last = tile([P, I], BF16, "v_last")
        turn(picked[3][:], v_last[:], nc.scalar.copy)
        quantise(w_grouped[1][:], w_codes[:, P:], w_scales[:, P:])
        quantise(v_third[:], v_codes[2][:], v_scales[2][:])
        quantise(v_last[:], v_codes[3][:], v_scales[3][:])
        v_mx = [(v_codes[t][:], v_scales[t][:]) for t in range(PACK)]

        def multiply(out, t, cols):
            nc.tensor.matmul_mx(
                out=out, lhsT=v_mx[t][0].bitcast(FP8X4), lhsT_scale=v_mx[t][1],
                rhs=w_codes[:, cols].bitcast(FP8X4), rhs_scale=w_scales[:, cols], start=True, stop=True,
            )

        o_codes = tile([P, Q], U32, "o_codes")
        o_scales = tile([P, Q], U8, "o_scales")
        out_rows = out_0.rearrange("(p t) q -> p t q", t=PACK)
        out_words = out_1[0].rearrange("p c t -> p (c t)").bitcast(I32)
        o_grouped = tile([P, Q, PACK], BF16, "o_grouped")
        o_sb = tile([P, PACK, Q], F32, "o_sb")
        halves = [slice(h * P, (h + 1) * P) for h in range(HALVES)]
        for cols in halves:
            bank = sums.tile([P, 2, P], F32, name="bank")
            for t in range(2):
                multiply(bank[:, t, :], t, cols)
            nc.scalar.copy(out=o_sb[:, :2, cols], in_=bank[:])
        nc.sync.dma_start(out=out_rows[:, :2, :], in_=o_sb[:, :2, :])
        bank = sums.tile([P, Q], F32, name="bank")
        multiply(bank[:], 2, slice(0, Q))
        nc.vector.tensor_copy(out=o_sb[:, 2, :], in_=bank[:])
        nc.sync.dma_start(out=out_rows[:, 2, :], in_=o_sb[:, 2, :])
        for cols in halves:
            bank = turns.tile([P, P], F32, name="turned")
            multiply(bank[:], 3, cols)
            nc.scalar.copy(out=o_sb[:, 3, cols], in_=bank[:])
        nc.sync.dma_start(out=out_rows[:, 3, :], in_=o_sb[:, 3, :])
        for copy, cols in (
            (nc.vector.tensor_copy, slice(0, P - GROUP_SHARE)), (nc.scalar.copy, slice(P - GROUP_SHARE, P)),
            (nc.vector.tensor_copy, halves[1]),
        ):
            copy(
                out=o_grouped[:, cols, :].rearrange("p (c i) t -> p c t i", i=4),
                in_=o_sb[:, :, cols].rearrange("p t (c i) -> p c t i", i=4),
            )
        for h in range(HALVES):
            cols = slice(h * P, (h + 1) * P)
            nc.vector.quantize_mx(
                out=o_codes[:, cols].bitcast(FP8X4), scales=o_scales[:, cols],
                in_=o_grouped[:, cols, :].rearrange("p q t -> p (q t)"),
            )
        nc.sync.dma_start(out=out_words, in_=o_codes[:].bitcast(I32))
        for quad in range(4):
            queue = nc.sync if quad % 2 == 0 else nc.scalar
            queue.dma_start(
                out=out_2[0, 4 * quad : 4 * quad + 4, :].bitcast(I32),
                in_=o_scales[32 * quad : 32 * quad + 4, :].bitcast(I32),
            )
